import numpy as np, ml_dtypes
CORES = [8,9,10,11,12,13]
N = 6
BF = ml_dtypes.bfloat16
W, L, S, J, TB, D = 4096, 128, 32, 32, 2, 3
NE = (TB + 1) // 2 * L
def cands(u, k):
    return ((u * u >> 5)[..., None] + (2 * np.arange(J) + 1) * u[..., None] + k) & (W - 1)
def pairs(rng, n, pen):
    s = np.arange(W) % S
    kv = rng.random(W) + pen * ((s < TB) & (s % 2 == 0)); ky = rng.random(W) + pen * ((s < TB) & (s % 2 == 1))
    row = np.full(W, -1, np.int64); row[rng.permutation(np.argsort(kv)[:n])] = np.argsort(ky)[:n]
    return row
def filled(rng, lo, hi):
    return np.stack([np.stack([pairs(rng, int(W * (lo + (hi - lo) * rng.random())), 0.6) for g in range(8)]) for r in range(N)])
def pack(x, a, w):
    b = np.full((N, 8, W), -1, np.int64)
    for r in range(N):
        for g in range(8):
            v = np.flatnonzero(a[r, g] >= 0); b[(r + 1) % N, g, a[r, g, v]] = v
    return {"x": np.ascontiguousarray(x).reshape(N, 128, W).astype(np.float32).astype(BF), "pa": a.astype(np.int32), "pb": b.astype(np.int32), "wt": np.ascontiguousarray(w).reshape(N, 128, 1).astype(np.int32)}
def some(rng, m):
    us = np.flatnonzero(m)
    return int(us[int(rng.integers(0, us.size))]) if us.size else 0
def hashed(z, w, u):
    z = np.array(z); z[:2] = 0; rho = (u - int(np.sum(w * z))) & (W - 1); z[0] = rho & 255; z[1] = rho >> 8
    return z
def firststep(x, a, w, r):
    q = (r + 1) % N; v = S * np.arange(L); z = x[r][:, :, v]; u = np.sum(w[q][:, :, None] * z, axis=1) & (W - 1); c = cands(u, 0)
    col = np.take_along_axis(x[q], c.reshape(8, 1, L * J), 2).reshape(8, 16, L, J); key = np.sum(np.abs(col - z[..., None]), axis=1) * W + c
    y = np.take_along_axis(c, np.argmin(key, axis=2)[..., None], 2)[..., 0]; taken = np.zeros((8, W), bool)
    for g in range(8): taken[g, a[r, g][a[r, g] >= 0]] = True
    return y, (a[r][:, v] < 0) & ~np.take_along_axis(taken, y, 1), taken
def setup_inputs(rng):
    return pack(rng.integers(0, 256, (N, 8, 16, W)), filled(rng, 0.4, 0.85), rng.integers(1, 4096, (N, 8, 16)))
def setup_inputs_spread(rng):
    x = np.minimum(np.exp2(8 * rng.random((N, 8, 1, W))) * rng.random((N, 8, 16, W)) * 1.25, 255).astype(np.int64) * (rng.random((N, 8, 1, W)) > 0.0625)
    w = np.minimum(np.maximum(np.exp2(12 * rng.random((N, 8, 16))).astype(np.int64), 1), 4095)
    return pack(x, filled(rng, 0.05, 0.95), w)
def setup_inputs_ties(rng):
    recs = rng.integers(0, 256, (1, 8, 16, 12)); recs[..., 0] = 0; recs[..., 1] = 0; recs[:, :, 0, 1] = 1
    pick = rng.integers(0, 12, (N, 8, W)); w = rng.integers(1, 4096, (N, 8, 16)); w[:, :, 0] = 2048
    x = np.take_along_axis(np.ascontiguousarray(np.broadcast_to(recs, (N, 8, 16, 12))), pick[:, :, None, :], 3)
    return pack(x, filled(rng, 0.3, 0.9), w)
def setup_inputs_corners(rng):
    x = rng.integers(0, 256, (N, 8, 16, W)); col = rng.random((N, 8, 1, W)); x = np.where(col < 0.06, 0, np.where(col > 0.94, 255, x))
    w = rng.integers(1, 4096, (N, 8, 16)); k = rng.integers(0, 4, (N, 8, 1)); w = np.where(k == 0, 1, np.where(k == 1, 4095, w))
    off = int(rng.integers(0, 8)); a = np.full((N, 8, W), -1, np.int64); s = np.arange(W)
    for r in range(N):
        for g in range(8):
            m = (r + g + off) % 8
            if m == 1: a[r, g] = rng.permutation(W)
            elif m == 2: a[r, g] = pairs(rng, W - NE, 2.0)
            elif m == 3: a[r, g, np.delete(s, W - S)] = rng.permutation(W - 1)
            elif m == 4 or m == 5:
                v = np.flatnonzero(pairs(rng, W // 2 if m == 4 else 3 * W // 4, 0.6) >= 0); a[r, g, v] = v if m == 4 else W - 1 - v
            elif m == 6:
                a[r, g] = pairs(rng, 3 * W // 4, 2.0); rec = rng.integers(0, 256, (16, 1))
                for t in range(0, TB, 2): x[r, g][:, t::S] = rec
    tab = cands(np.arange(W), 0); starter = (s % S < TB) & (s % S % 2 == 0)
    for r in range(N):
        g = (7 - r - off) % 8; q = (r + 1) % N; w[q, g, 0] = 1; w[q, g, 1] = 256
        lanes = np.concatenate([np.arange(0, 32, 2 - r % 2), np.arange(32, 96)]); pl = np.where(lanes < 32, 97 + lanes, 128 + lanes)
        held = a[r - 1, g]; held = held[held >= 0]; held = held[held % S >= TB]; h = rng.permutation(held)[:lanes.size]
        row = np.full(W, -1, np.int64); row[h] = pl[:h.size]; fv = ~starter; fv[h] = False; fy = np.ones(W, bool); fy[96:129] = False; fy[160:224] = False
        row[rng.permutation(np.flatnonzero(fv))[:W // 2]] = rng.permutation(np.flatnonzero(fy))[:W // 2]; a[r, g] = row
        for e in range(h.size):
            k = int(lanes[e]); P = int(pl[e]); z = hashed(rng.integers(0, 256, 16), w[q, g], some(rng, np.any(tab == P, axis=1)))
            if k < 32: there = z; back = np.zeros(16, np.int64)
            else:
                kk = (k - 32) >> 1 if r % 2 == 1 else 2 * ((k - 32) >> 2)
                hit = ((tab + 97 + kk) & (W - 1)) == P; there = hashed(z, w[q, g], some(rng, np.any(hit, axis=1) & ~np.all(hit, axis=1))); back = there
            x[r, g][:, S * k] = z; x[q, g][:, P] = there; x[r, g][:, int(h[e])] = back
    for r in range(0, N, 2):
        g = (7 - r - off) % 8; y, go, taken = firststep(x, a, w, r); n = 0
        for b in range(8): n = n + int(np.unique(y[b][go[b]]).size)
        if n % 2 == 1:
            cnt = np.bincount(y[g][go[g]], minlength=W); one = np.flatnonzero(go[g] & (cnt[y[g]] == 1) & (np.arange(L) >= 96))
            fr = ~taken[g]; fr[y[g]] = False; fr[96:129] = False; fr[160:224] = False; fr = np.flatnonzero(fr)
            if one.size and fr.size: a[r, g, S * int(one[int(rng.integers(0, one.size))])] = int(fr[int(rng.integers(0, fr.size))])
    return pack(x, a, w)
def setup_inputs_ends(rng):
    kind = (7 - np.arange(8)[None, :] + N - 1 - np.arange(N)[:, None]) % 4
    w = np.where(rng.random((N, 8, 16)) < 0.5, 1, 4095); w[kind == 0] = 4095; w[kind == 3] = 1
    x = 255 * (rng.random((N, 8, 16, W)) < rng.choice(np.array([0.0, 0.25, 0.5, 0.75, 1.0]), (N, 8, 1, W))).astype(np.int64)
    pick = rng.random((N, 8, L)) < 0.25; pick[:, :, L - 1] = True; x[:, :, :, ::S] = np.where(pick[:, :, None, :], 255, x[:, :, :, ::S])
    tab = cands(np.arange(W), 0); top = np.max(tab, axis=1); pool = np.flatnonzero(top == np.max(top))
    a = np.full((N, 8, W), -1, np.int64); n = 3 * W // 8
    for r in range(N):
        for g in range(8):
            if kind[r, g] == 1:
                need = int(pool[int(rng.integers(0, pool.size))]) * 3839; i = int(rng.integers(0, 16)); o = (i + 1) % 16; w[r, g, i] = 0
                if (need - int(np.sum(w[r, g]))) & (W - 1) == 0: w[r, g, o] = 4096 - w[r, g, o]
                w[r, g, i] = (need - int(np.sum(w[r, g]))) & (W - 1)
            c = cands(np.array([255 * int(np.sum(w[r, g])) & (W - 1)]), 0)[0]; c = c[c % S != 0]
            if c.size:
                x[r, g][:, c] = 0
                if kind[r, g] == 2: x[r, g][:, int(np.max(c))] = 255
            v = rng.permutation(W); v = v[(v != 0) & (v != W - 1) & (v != W - S)][:n]; y = rng.permutation(W); y = y[(y != 0) & (y != W - 1)][:n]
            a[r, g, v] = y
            if g % 2 == 0: a[r, g, 0] = W - 1; a[r, g, W - 1] = 0
    return pack(x, a, w)
def setup_inputs_paths(rng):
    x = rng.integers(0, 256, (N, 8, 16, W)); w = rng.integers(1, 4096, (N, 8, 16)); w[:, :, 0] = 1; w[:, :, 1] = 256
    tab = cands(np.arange(W), 0); s = np.arange(W); gs = rng.permutation(8); lanes = np.argsort(rng.random((N, 8, L)), axis=-1); cnt = np.zeros((N, 8), np.int64)
    use = np.zeros((N, 8, W), bool); use[:, :, s % S < TB] = True; use[:, :, 1850:1920] = True; use[:, :, 3770:3840] = True
    for o in range(0, W, 1024): use[:, :, o + 96:o + 256] = True
    fv = [[[] for g in range(8)] for r in range(N)]; fy = [[[] for g in range(8)] for r in range(N)]; link = [[[] for g in range(8)] for r in range(N)]
    k0 = np.zeros(N, np.int64); k1 = np.zeros(N, np.int64)
    def start(r, g):
        v = S * int(lanes[r, g, cnt[r, g]]); cnt[r, g] += 1; fv[r][g].append(v)
        return v
    def spot(r, g):
        c = np.flatnonzero(~use[r, g]); p = int(c[int(rng.integers(0, c.size))]); use[r, g, p] = True
        return p
    def reach(r, g, k, v=None, u=0):
        z = rng.integers(0, 256, 16)
        for e in range(40):
            z = rng.integers(0, 256, 16)
            if v is not None: z = hashed(z, v, u)
            c = cands(np.array([int(np.sum(w[r, g] * z)) & (W - 1)]), k)[0]; c = c[~use[r, g, c]]
            if c.size:
                p = int(c[int(rng.integers(0, c.size))]); use[r, g, p] = True
                return z, p
        return z, -1
    def visit(r, g, P, rec, b):
        q = (r + 1) % N; m = np.any(tab == P, axis=1)
        if not np.any(m): return None
        z = hashed(rng.integers(0, 256, 16), w[q, g], some(rng, m)); v = start(r, g)
        if b < 0: b = spot(r, g)
        x[r, g][:, v] = z; x[q, g][:, P] = z; x[r, g][:, b] = rec; link[r][g].append((b, P))
        return z
    for r in range(N):
        q = (r + 1) % N; g = int(gs[0])
        for i in range(L):
            z, p = reach(q, g, 0)
            if p >= 0: x[r, g][:, S * i] = z; x[q, g][:, p] = z; fv[r][g].append(S * i); fy[r][g].append(p); k0[q] += 1
        g = int(gs[1]); xq = x[q, g]
        z = hashed(rng.integers(200, 256, 16), w[q, g], 4095); x[r, g][:, start(r, g)] = z; c = cands(np.array([4095]), 0)[0]
        j = 2 * int(rng.integers(1, J // 2)); xq[:, c] = 0; xq[5, c[j]] = 8; xq[5, c[j - 1]] = 8; fy[r][g].append(int(c[j])); fy[r][g].append(int(c[j - 1]))
        z = hashed(rng.integers(200, 256, 16), w[q, g], 2047); x[r, g][:, start(r, g)] = z; c = cands(np.array([2047]), 0)[0]
        xq[:, c] = 0; xq[6, c] = (int(np.sum(z)) - 4) & 15; xq[5, c[0]] = 1; fy[r][g].append(int(c[0])); k0[q] += 2
    ka = [int(k) & 31 for k in k0]
    for r in range(N):
        q = (r + 1) % N; g = int(gs[2])
        if q % 2 == 1:
            w[q, g, 2] = 0; need = (1024 + 2048 * int(rng.integers(0, 2))) * 3839
            if (need - int(np.sum(w[q, g]))) & (W - 1) == 0: w[q, g, 3] += 1 if w[q, g, 3] < 4095 else -1
            w[q, g, 2] = (need - int(np.sum(w[q, g]))) & (W - 1)
            if visit(r, g, 1024 + 97 + ka[q], np.full(16, 255, np.int64), -1) is not None:
                x[q, g][:, 3072 + 97 + ka[q]] = 0; fy[r][g].append(3072 + 97 + ka[q]); k1[q] += 1
        g = int(gs[4])
        if r % 2 == 1:
            for o in (0, 2048):
                rb, b = reach(r, g, 97 + ka[r], w[q, g], o); z, p = reach(r, g, 0)
                if b >= 0 and p >= 0 and visit(r, g, o + 97 + ka[q], rb, b) is not None:
                    fy[r][g].append(o + 194); v = start(r - 1, g); e = spot(r - 1, g)
                    x[r - 1, g][:, v] = z; x[r, g][:, p] = z; x[r - 1, g][:, e] = rb; link[r - 1][g].append((e, p)); fy[r - 1][g].append(b); k1[r] += 1
    kb = [int(k) & 31 for k in k1]
    for r in range(N):
        q = (r + 1) % N; g = int(gs[3])
        for o in (0, 2048):
            if visit(r, g, o + 97 + ka[q], hashed(rng.integers(0, 256, 16), w[q, g], o), -1) is not None: fy[r][g].append(o + 194 + kb[q])
        g = int(gs[5]); z1, p = reach(q, g, 97 + ka[q])
        if p >= 0:
            z = visit(r, g, 1024 + 194 + kb[q], z1, -1)
            if z is not None:
                z = hashed(z, w[q, g], 1024); b = spot(r, g); x[q, g][:, p] = z1; x[r, g][:, b] = z; link[r][g].append((b, p))
                x[q, g][:, 3072 + 194 + kb[q]] = np.where(z < 128, 255, 0); fy[r][g].append(3072 + 194 + kb[q])
    a = np.full((N, 8, W), -1, np.int64)
    for r in range(N):
        for g in range(8):
            mv = np.ones(W, bool); my = np.ones(W, bool); mv[np.array(fv[r][g], np.int64)] = False; my[np.array(fy[r][g], np.int64)] = False
            for v, y in link[r][g]: mv[v] = False; my[y] = False; a[r, g, v] = y
            vs = np.flatnonzero(mv); vs = np.concatenate([vs[vs % S == 0], rng.permutation(vs[vs % S != 0])[:W // 2]])
            a[r, g, vs] = rng.permutation(np.flatnonzero(my))[:vs.size]
    return pack(x, a, w)
def check_inputs(d):
    bad = []; xx = np.asarray(d["x"]).astype(np.float32)
    if not (np.min(xx) >= 0 and np.max(xx) <= 255): bad.append("range of x")
    if np.any(xx != np.floor(xx)): bad.append("x not whole")
    for k, lo, hi in (("pa", -1, W - 1), ("pb", -1, W - 1), ("wt", 1, 4095)):
        if not (np.min(d[k]) >= lo and np.max(d[k]) <= hi): bad.append("range of " + k)
    own = np.arange(W)[None, :]; off = False
    for r in range(N):
        a = np.asarray(d["pa"])[r].astype(np.int64); b = np.asarray(d["pb"])[(r + 1) % N].astype(np.int64)
        for c, e in ((a, b), (b, a)):
            if np.any((c >= 0) & (np.take_along_axis(e, np.clip(c, 0, W - 1), 1) != own)): off = True
    if off: bad.append("pa and pb not mutual")
    return bad
def reference(x, pa, pb, wt):
    X = x.astype(np.float32).astype(np.int32).reshape(N, 8, 16, W); A = pa.astype(np.int64); B = pb.astype(np.int64); w = wt.astype(np.int64).reshape(N, 8, 16, 1)
    kap = np.zeros(N, np.int64); lane = np.arange(L)
    for t in range(TB):
        q = (np.arange(N) + (1 if t % 2 == 0 else -1)) % N
        near, far = (A, B) if t % 2 == 0 else (B, A)
        v = S * lane + t; x0 = X[:, :, :, v]; z = x0; live = near[:, :, v] < 0; last = np.full((N, 8, L), -1, np.int64)
        for d in range(D):
            u = np.sum(w[q] * z, axis=2) & (W - 1)
            c = cands(u, (97 * d + kap[q])[:, None, None, None])
            col = np.take_along_axis(X[q], c.reshape(N, 8, 1, L * J), 3).reshape(N, 8, 16, L, J)
            dist = np.sum(np.abs(col - z[..., None]), axis=2)
            key = np.where(c == last[..., None], 2 ** 24, dist.astype(np.int64) * W + c)
            y = np.take_along_axis(c, np.argmin(key, axis=3)[..., None], 3)[..., 0]
            go = live & (np.take_along_axis(far[q], y, 2) < 0)
            rr, gg, ii = np.nonzero(go); low = np.full((N, 8, W), L, np.int64); np.minimum.at(low, (rr, gg, y[go]), ii)
            win = go & (np.take_along_axis(low, y, 2) == lane)
            rr, gg, ii = np.nonzero(win); yy = y[win]; qq = q[rr]; vv = S * ii + t
            X[qq, gg, :, yy] = (X[qq, gg, :, yy] + x0[rr, gg, :, ii]) >> 1
            far[qq, gg, yy] = vv; near[rr, gg, vv] = yy
            live = live & ~win; kap = np.bincount(qq, minlength=N).astype(np.int64) & 31; last = y
            p = np.maximum(np.take_along_axis(far[q], y, 2), 0)
            z = np.where(live[:, :, None, :], np.take_along_axis(X, p[:, :, None, :], 3), z)
    return {"yx": X.reshape(N, 128, W).astype(np.float32).astype(BF), "ya": A.astype(np.float32), "yb": B.astype(np.float32)}

@@ -1,0 +1,521 @@
+from concourse.mybir import dt, AluOpType, AxisListType, ActivationFunctionType
+
+A = AluOpType
+AF = ActivationFunctionType
+W, L, TB, D = 4096, 128, 2, 3
+WX = W + L
+FULL = 16777216.0
+
+SCRATCH = {
+    "X": ("sbuf", [128, WX], "bfloat16"),
+    "XR0": ("sbuf", [128, WX], "bfloat16"),
+    "XR1": ("sbuf", [128, WX], "bfloat16"),
+    "FA": ("sbuf", [128, WX], "float32"),
+    "FB": ("sbuf", [128, WX], "float32"),
+    "P8": ("sbuf", [8, W], "int32"),
+    "PA2": ("sbuf", [128, 256], "int32"),
+    "PB2": ("sbuf", [128, 256], "int32"),
+    "PA2F": ("sbuf", [128, 256], "float32"),
+    "PB2F": ("sbuf", [128, 256], "float32"),
+    "da": ("dram", [8, W], "float32"),
+    "db": ("dram", [8, W], "float32"),
+    "WTI": ("sbuf", [128, 1], "int32"),
+    "WHI": ("sbuf", [128, 1], "int32"),
+    "WLI": ("sbuf", [128, 1], "int32"),
+    "WF": ("sbuf", [128, 2], "float32"),
+    "WH": ("sbuf", [128, 128], "bfloat16"),
+    "WL": ("sbuf", [128, 128], "bfloat16"),
+    "PI": ("sbuf", [128, 1], "int32"),
+    "PMI": ("sbuf", [128, 1], "int32"),
+    "PGI": ("sbuf", [128, 1], "int32"),
+    "PF": ("sbuf", [128, 3], "float32"),
+    "CI": ("sbuf", [128, 128], "int32"),
+    "CMI": ("sbuf", [128, 128], "int32"),
+    "CGI": ("sbuf", [128, 128], "int32"),
+    "M16": ("sbuf", [128, 128], "float32"),
+    "M16M": ("sbuf", [128, 128], "float32"),
+    "BOB": ("sbuf", [128, 128], "bfloat16"),
+    "BOF": ("sbuf", [128, 128], "float32"),
+    "IDF": ("sbuf", [128, 128], "float32"),
+    "NID": ("sbuf", [128, 128], "bfloat16"),
+    "ONF": ("sbuf", [128, 128], "float32"),
+    "SEL8": ("sbuf", [128, 8], "float32"),
+    "GM8": ("sbuf", [128, 8], "bfloat16"),
+    "GMF": ("sbuf", [128, 128], "float32"),
+    "GMX": ("sbuf", [128, 128], "bfloat16"),
+    "E8": ("sbuf", [8, 128], "bfloat16"),
+    "BJ": ("sbuf", [128, 2], "float32"),
+    "BJ2": ("sbuf", [128, 2], "float32"),
+    "KB": ("sbuf", [128, 2], "float32"),
+    "KC": ("sbuf", [128, 2], "float32"),
+    "ZD0": ("sbuf", [128, 128], "float32"),
+    "RS0": ("sbuf", [128, 128], "float32"),
+    "RS": ("sbuf", [128, 128], "float32"),
+    "HALF": ("sbuf", [128, 128], "float32"),
+    "ZERO": ("sbuf", [128, 128], "float32"),
+    "PW": ("sbuf", [128, 128], "float32"),
+    "PWM": ("sbuf", [128, 128], "float32"),
+    "PWS": ("sbuf", [128, 128], "float32"),
+    "DW0": ("sbuf", [128, 8], "float32"),
+    "DW": ("sbuf", [128, 8], "float32"),
+    "ST0": ("sbuf", [128, 128], "float32"),
+    "ST1": ("sbuf", [128, 128], "float32"),
+    "LV8": ("sbuf", [8, 128], "bfloat16"),
+    "LS0": ("sbuf", [128, 128], "float32"),
+    "LS1": ("sbuf", [128, 256], "float32"),
+    "LSF": ("sbuf", [128, 128], "float32"),
+    "LL0": ("sbuf", [128, 128], "float32"),
+    "LL1": ("sbuf", [128, 256], "float32"),
+    "LLF": ("sbuf", [128, 128], "float32"),
+    "SN0": ("sbuf", [128, 128], "bfloat16"),
+    "SN1": ("sbuf", [128, 128], "bfloat16"),
+    "SS0": ("sbuf", [128, 128], "bfloat16"),
+    "SS1": ("sbuf", [128, 128], "bfloat16"),
+    "RT": ("sbuf", [128, 128], "float32"),
+    "RSC": ("sbuf", [128, 128], "float32"),
+    "RW": ("sbuf", [128, 8], "float32"),
+    "RWT": ("sbuf", [128, 8], "float32"),
+    "Z": ("sbuf", [128, 128], "bfloat16"),
+    "ZR": ("sbuf", [128, 2048], "bfloat16"),
+    "UI": ("sbuf", [128, 128], "int32"),
+    "UM": ("sbuf", [128, 128], "int32"),
+    "UF": ("sbuf", [128, 128], "float32"),
+    "SQ": ("sbuf", [128, 256], "float32"),
+    "AI": ("sbuf", [128, 256], "int32"),
+    "CC": ("sbuf", [128, 256], "int32"),
+    "CU": ("sbuf", [128, 256], "uint16"),
+    "CF": ("sbuf", [128, 256], "float32"),
+    "NQ": ("sbuf", [128, 256], "bfloat16"),
+    "DD": ("sbuf", [128, W], "bfloat16"),
+    "R0": ("sbuf", [128, 128], "float32"),
+    "R1": ("sbuf", [128, 128], "float32"),
+    "MK": ("sbuf", [128, 8], "float32"),
+    "MI": ("sbuf", [128, 8], "int32"),
+    "ZS": ("sbuf", [128, 128], "int32"),
+    "YE": ("sbuf", [128, 128], "float32"),
+    "YM": ("sbuf", [128, 128], "float32"),
+    "YU": ("sbuf", [128, 8], "uint16"),
+    "YD": ("sbuf", [128, 8], "float32"),
+    "EL": ("sbuf", [128, 128], "float32"),
+    "TH": ("sbuf", [128, 128], "float32"),
+    "EQ": ("sbuf", [128, 1024], "bfloat16"),
+    "XG": ("sbuf", [128, 128], "float32"),
+    "NR": ("sbuf", [128, 128], "int32"),
+    "WM": ("sbuf", [128, 128], "float32"),
+    "WS": ("sbuf", [128, 128], "float32"),
+    "SF0": ("sbuf", [128, 8], "float32"),
+    "SF": ("sbuf", [128, 8], "float32"),
+    "Y1": ("sbuf", [128, 128], "float32"),
+    "YA": ("sbuf", [128, 128], "float32"),
+    "YN": ("sbuf", [128, 128], "float32"),
+    "CT": ("sbuf", [128, 1], "float32"),
+    "KI": ("sbuf", [128, 1], "int32"),
+    "KJ": ("sbuf", [128, 1], "int32"),
+    "KF": ("sbuf", [128, 1], "float32"),
+    "PG": ("sbuf", [128, 128], "float32"),
+    "PS": ("sbuf", [128, 128], "float32"),
+    "PU": ("sbuf", [128, 8], "uint16"),
+    "pU": ("psum", [128, 512], "float32"),
+    "pK0": ("psum", [128, 512], "float32"),
+    "pK1": ("psum", [128, 512], "float32"),
+    "pYR": ("psum", [128, 512], "float32"),
+    "pYW": ("psum", [128, 512], "float32"),
+    "pWS": ("psum", [128, 512], "float32"),
+    "pC": ("psum", [128, 512], "float32"),
+    "pM": ("psum", [128, 512], "float32"),
+}
+for _t in range(TB):
+    for _d in range(D):
+        SCRATCH["MU%d%d" % (_t, _d)] = ("sbuf", [128, 136], "uint16")
+        if _d < D - 1:
+            SCRATCH["UL%d%d" % (_t, _d)] = ("sbuf", [128, 136], "uint16")
+
+REMOTE = ["L0", "S0", "X0", "U00", "U01", "S1", "L1", "X1", "U10", "U11", "LF"]
+LOCAL = ["dW", "dP8", "dX", "dPB", "dPA", "dDB", "dDA", "dFB", "dFA", "oX", "oA", "oB"]
+SEMAPHORES = ["qV", "qS", "qT", "qG"] + ["a" + n for n in REMOTE] + ["l" + n for n in REMOTE] + LOCAL
+
+
+def machine(g, core, T, topo):
+    Q = {"V": g.vector, "S": g.scalar, "T": g.tensor, "G": g, "Y": g.sync}
+    sem = {"V": "qV", "S": "qS", "T": "qT", "G": "qG"}
+    cnt = {}
+    know = {q: {} for q in Q}
+    snap = {}
+    lastw = {}
+    readers = {}
+
+    def wait(q, toks):
+        todo = []
+        for t in toks:
+            if t not in todo and know[q].get(t[0], 0) < t[1]:
+                todo.append(t)
+        keep = []
+        for t in todo:
+            covered = False
+            for o in todo:
+                if o != t and snap.get(o, {}).get(t[0], 0) >= t[1]:
+                    covered = True
+            if not covered:
+                keep.append(t)
+        for s, v in keep:
+            if know[q].get(s, 0) >= v:
+                continue
+            Q[q].wait_ge(T.sem[s], v)
+            know[q][s] = max(know[q].get(s, 0), v)
+            for a, b in snap.get((s, v), {}).items():
+                know[q][a] = max(know[q].get(a, 0), b)
+
+    def deps(q, reads, writes):
+        toks = []
+        for r in reads:
+            if r in lastw:
+                toks.append(lastw[r][0])
+        for w in writes:
+            if w in lastw and not (q == "T" and lastw[w][1] == "T"):
+                toks.append(lastw[w][0])
+            toks.extend(readers.get(w, []))
+        wait(q, toks)
+
+    def book(q, tok, reads, writes):
+        for r in reads:
+            old = [t for t in readers.get(r, []) if t[0] != tok[0]]
+            readers[r] = old + [tok]
+        for w in writes:
+            lastw[w] = (tok, q)
+            readers[w] = []
+
+    def op(q, reads, writes, *fns):
+        deps(q, reads, writes)
+        ins = None
+        for f in fns:
+            ins = f()
+        cnt[sem[q]] = cnt.get(sem[q], 0) + 1
+        ins.then_inc(T.sem[sem[q]], 1)
+        tok = (sem[q], cnt[sem[q]])
+        know_now = dict(know[q])
+        know_now[sem[q]] = tok[1]
+        snap[tok] = know_now
+        book(q, tok, reads, writes)
+
+    def dma(q, name, pairs, reads, writes):
+        deps(q, reads, writes)
+        for o, i in pairs:
+            Q[q].dma_start(o, i).then_inc(T.sem[name], 16)
+        cnt[name] = 16 * len(pairs)
+        tok = (name, cnt[name])
+        snap[tok] = dict(know[q])
+        book(q, tok, reads, writes)
+
+    def send(name, dst, out, src, reads, lands):
+        deps("G", reads, [])
+        rid, pid = topo.addr(dst)[0], topo.addr(dst)[1]
+        g.remote_dma(out_ap=out, in_ap=src, remote_sem=T.sem["a" + name], local_sem=T.sem["l" + name],
+                     pid=pid, routing_id=rid, dma_engine_mask=topo.mask(core, dst))
+        n = len(topo.engines(core, dst))
+        cnt["l" + name] = n
+        cnt["a" + name] = n
+        book("G", ("l" + name, n), reads, [])
+        lastw[lands] = (("a" + name, n), "R")
+        readers[lands] = []
+
+    def finish():
+        wait("G", [(s, n) for s, n in cnt.items()])
+
+    return op, dma, send, finish
+
+
+def rank_program(g, core, T, topo):
+    rank = T.rank_of(core)
+    if rank is None:
+        return
+    N = len(T.cores)
+    nxt, prv = T.cores[(rank + 1) % N], T.cores[(rank - 1) % N]
+    op, dma, send, finish = machine(g, core, T, topo)
+    V, S, TE = g.vector, g.scalar, g.tensor
+
+    def ts(reads, writes, out, in0, s1, o0, s2=None, o1=None):
+        if o1 is None:
+            op("V", reads, writes, lambda: V.tensor_scalar(out, in0, s1, None, o0))
+        else:
+            op("V", reads, writes, lambda: V.tensor_scalar(out, in0, s1, s2, o0, o1))
+
+    def tt(reads, writes, out, in0, in1, o):
+        op("V", reads, writes, lambda: V.tensor_tensor(out, in0, in1, o))
+
+    def cp(reads, writes, out, in_):
+        op("V", reads, writes, lambda: V.tensor_copy(out, in_))
+
+    def scan(reads, writes, out, d0, d1, init, o0, o1):
+        op("V", reads, writes, lambda: V.tensor_tensor_scan(out, d0, d1, init, o0, o1))
+
+    def fill(writes, ap, c):
+        op("V", [], writes, lambda: V.memset(ap, c))
+
+    def mm(out, lhsT, rhs, start=True, stop=True):
+        return lambda: TE.matmul(out, lhsT, rhs, start, stop)
+
+    dma("Y", "dP8", [(T.P8[:], T.pa[:])], [], ["P8"])
+    dma("Y", "dX", [(T.X[:, 0:W], T.x[:])], [], ["X"])
+    dma("Y", "dW", [(T.WTI[:], T.wt[:])], [], ["WTI"])
+    dma("Y", "dPB", [(T.PB2[:], T.pb[:])], [], ["PB2"])
+    dma("Y", "dPA", [(T.PA2[:], T.pa[:])], [], ["PA2"])
+
+    op("G", [], ["PI"], lambda: g.iota(T.PI[:], [[0, 1]], 0, 1))
+    op("G", [], ["CI"], lambda: g.iota(T.CI[:], [[1, 128]], 0, 0))
+    fill(["ONF"], T.ONF[:], 1.0)
+    fill(["HALF"], T.HALF[:], 0.5)
+    fill(["ZERO"], T.ZERO[:], 0.0)
+    fill(["ZSc"], T.ZS[:], 0)
+    for n in ("X", "XR0", "XR1", "FA", "FB"):
+        fill([n + "spare"], T[n][:, W:WX], 0.0)
+    ts(["PI"], ["PMI"], T.PMI[:], T.PI[:], 15, A.bitwise_and)
+    ts(["PI"], ["PGI"], T.PGI[:], T.PI[:], 4, A.logical_shift_right)
+    ts(["CI"], ["CMI"], T.CMI[:], T.CI[:], 15, A.bitwise_and)
+    ts(["CI"], ["CGI"], T.CGI[:], T.CI[:], 4, A.logical_shift_right)
+    cp(["PI"], ["PFp"], T.PF[:, 0:1], T.PI[:])
+    cp(["PMI"], ["PFm"], T.PF[:, 1:2], T.PMI[:])
+    cp(["PGI"], ["PFg"], T.PF[:, 2:3], T.PGI[:])
+    P_, PM, PGc = T.PF[:, 0:1], T.PF[:, 1:2], T.PF[:, 2:3]
+    ts(["CGI", "PFp"], ["E8"], T.E8[:], T.CGI[0:8, :], T.PF[0:8, 0:1], A.is_equal)
+    ts(["CMI", "PFm"], ["M16"], T.M16[:], T.CMI[:], PM, A.is_equal)
+    ts(["P8"], ["LV8"], T.LV8[:], T.P8[:, 0:W:32], 0.0, A.is_lt)
+    op("T", ["E8", "LV8"], ["pM"], mm(T.pM[:, 0:128], T.E8[:], T.LV8[:]))
+    ts(["CGI", "PFg"], ["BOB"], T.BOB[:], T.CGI[:], PGc, A.is_equal)
+    ts(["CGI", "PFg"], ["BOF"], T.BOF[:], T.CGI[:], PGc, A.is_equal)
+    tt(["pM", "M16"], ["LS0"], T.LS0[:], T.pM[:, 0:128], T.M16[:], A.mult)
+    send("L0", nxt, T.LL0[:], T.LS0[:], ["LS0"], "LL0")
+    ts(["WTI"], ["WHI"], T.WHI[:], T.WTI[:], 4032, A.bitwise_and)
+    ts(["WTI"], ["WLI"], T.WLI[:], T.WTI[:], 63, A.bitwise_and)
+    cp(["WHI"], ["WFh"], T.WF[:, 0:1], T.WHI[:])
+    cp(["WLI"], ["WFl"], T.WF[:, 1:2], T.WLI[:])
+    ts(["BOB", "WFh"], ["WH"], T.WH[:], T.BOB[:], T.WF[:, 0:1], A.mult)
+    ts(["BOB", "WFl"], ["WL"], T.WL[:], T.BOB[:], T.WF[:, 1:2], A.mult)
+    ts(["PFm"], ["BJa"], T.BJ[:, 0:1], PM, 32.0, A.mult, 16.0, A.add)
+    ts(["PFm"], ["BJb"], T.BJ[:, 1:2], PM, 32.0, A.mult, 528.0, A.add)
+    tt(["BJa", "BJb"], ["BJ2"], T.BJ2[:], T.BJ[:], T.BJ[:], A.mult)
+    ts(["BJ2"], ["KB"], T.KB[:], T.BJ2[:], -1.0 / 32, A.mult, -0.4375, A.add)
+    cp(["X"], ["SN0"], T.SN0[:], T.X[:, 0:W:32])
+    send("S0", nxt, T.SS0[:], T.SN0[:], ["SN0"], "SS0")
+    send("X0", nxt, T.XR0[:, 0:W], T.X[:, 0:W], ["X"], "XR0")
+    cp(["PB2"], ["PB2F"], T.PB2F[:], T.PB2[:])
+    cp(["PA2"], ["PA2F"], T.PA2F[:], T.PA2[:])
+    dma("Y", "dDB", [(T.db[:], T.PB2F[:])], ["PB2F"], ["db"])
+    dma("Y", "dFB", [(T.FB[f:128:16, 0:W], T.db[:]) for f in range(16)], ["db"], ["FB"])
+    dma("Y", "dDA", [(T.da[:], T.PA2F[:])], ["PA2F"], ["da"])
+    dma("Y", "dFA", [(T.FA[f:128:16, 0:W], T.da[:]) for f in range(16)], ["da"], ["FA"])
+    ts(["CI", "PFp"], ["IDF"], T.IDF[:], T.CI[:], P_, A.is_equal)
+    ts(["CI", "PFp"], ["NID"], T.NID[:], T.CI[:], P_, A.is_equal, -FULL, A.mult)
+    ts(["CI", "PFg"], ["SEL8"], T.SEL8[:], T.CI[:, 0:8], PGc, A.is_equal)
+    ts(["CI", "PFg"], ["GM8"], T.GM8[:], T.CI[:, 0:8], PGc, A.is_equal, 4096.0, A.mult)
+    ts(["CMI"], ["GMF"], T.GMF[:], T.CMI[:], 15.0, A.is_equal, 4096.0, A.mult)
+    tt(["GMF", "BOF"], ["GMX"], T.GMX[:], T.GMF[:], T.BOF[:], A.mult)
+    ts(["M16"], ["M16M"], T.M16M[:], T.M16[:], -1.0, A.add)
+    ts(["CMI"], ["ZD0"], T.ZD0[:], T.CMI[:], 0.0, A.is_gt)
+    ts(["CMI"], ["RS0"], T.RS0[:], T.CMI[:], 0.0, A.is_equal, 1.0e8, A.mult)
+    ts(["RS0"], ["RS"], T.RS[:], T.RS0[:], -5.0e7, A.add)
+    scan(["HALF", "ZERO"], ["PW"], T.PW[:], T.HALF[:], T.ZERO[:], 2.0 ** 64, A.mult, A.add)
+    cp(["M16"], ["pC"], T.pC[:, 0:128], T.M16[:])
+    ts(["PW"], ["pC"], T.pC[:, 128:256], T.PW[:], 2.5, A.mult)
+    tt(["PW", "M16"], ["PWM"], T.PWM[:], T.PW[:], T.M16[:], A.mult)
+    scan(["PWM", "ZD0"], ["PWS"], T.PWS[:], T.ZD0[:], T.PWM[:], 0.0, A.mult, A.add)
+    ts(["CI", "PFm"], ["DW0"], T.DW0[:], T.CI[:, 0:8], 16.0, A.mult, PM, A.add)
+    ts(["DW0"], ["DW"], T.DW[:], T.DW0[:], float(W), A.add)
+    ts(["CI"], ["ST0"], T.ST0[:], T.CI[:], 32.0, A.mult)
+    ts(["CI"], ["ST1"], T.ST1[:], T.CI[:], 32.0, A.mult, 1.0, A.add)
+
+    M16P, THRP = T.pC[:, 0:128], T.pC[:, 128:256]
+
+    for t in range(TB):
+        far = "FB" if t == 0 else "FA"
+        F = T[far]
+        xr = "XR%d" % t
+        XR = T[xr]
+        ss = "SS%d" % t
+        SS = T[ss]
+        ll = "LL%d" % t
+        LL = T[ll]
+        ST = T["ST%d" % t]
+        to = nxt if t == 0 else prv
+        home = prv if t == 0 else nxt
+        for d in range(D):
+            zn = ss if d == 0 else "Z"
+            Z = T[zn]
+            op("T", ["WH", "WL", zn], ["pU"], mm(T.pU[:, 0:128], T.WH[:], Z[:], True, False),
+               mm(T.pU[:, 0:128], T.WL[:], Z[:], False, True))
+
+            def rep_v(m):
+                cp([zn], ["ZR%d" % m], T.ZR[:, m:2048:16], Z[:])
+
+            for m in range(8, 16):
+                op("S", [zn], ["ZR%d" % m],
+                   lambda: S.activation(T.ZR[:, m:2048:16], Z[:], AF.Copy))
+            for m in range(0, 4):
+                rep_v(m)
+            cp(["pU"], ["UI"], T.UI[:], T.pU[:, 0:128])
+            ts(["UI"], ["UM"], T.UM[:], T.UI[:], W - 1, A.bitwise_and)
+            cp(["UM"], ["UF"], T.UF[:], T.UM[:])
+            for b in range(2):
+                op("S", ["UF", "BJa", "BJb"], ["SQ%d" % b],
+                   lambda: S.activation(T.SQ[:, 128 * b:128 * b + 128], T.UF[:], AF.Square, bias=T.BJ[:, b:b + 1]))
+            for m in range(4, 8):
+                rep_v(m)
+            first = t == 0 and d == 0
+            KN = "KB" if first else "KC"
+
+            def lists(b):
+                c = slice(128 * b, 128 * b + 128)
+                ts(["SQ%d" % b, KN], ["AI%d" % b], T.AI[:, c], T.SQ[:, c], 1.0 / 32, A.mult, T[KN][:, b:b + 1], A.add)
+                ts(["AI%d" % b], ["CC%d" % b], T.CC[:, c], T.AI[:, c], W - 1, A.bitwise_and)
+                cp(["CC%d" % b], ["CU%d" % b], T.CU[:, c], T.CC[:, c])
+
+            def places(b):
+                c = slice(128 * b, 128 * b + 128)
+                cp(["CC%d" % b], ["CF%d" % b], T.CF[:, c], T.CC[:, c])
+                if d > 0:
+                    tt(["CC%d" % b, "pYR"], ["NQ%d" % b], T.NQ[:, c], T.CC[:, c], T.pYR[:, 0:128], A.not_equal)
+                pk = T["pK%d" % b]
+                op("T", ["CF%d" % b, "IDF"], ["pK%d" % b], mm(pk[:, 0:128], T.CF[:, c], T.IDF[:], True, False))
+                if d > 0:
+                    op("T", ["NQ%d" % b, "NID"], ["pK%d" % b], mm(pk[:, 0:128], T.NQ[:, c], T.NID[:], False, False))
+
+            zr_all = ["ZR%d" % m for m in range(16)]
+
+            def gather(b, lo, hi):
+                o, e = 2048 * b + 16 * lo, 2048 * b + 16 * hi
+                rg = "DD%d_%d" % (b, lo)
+                tt(["X", "CU%d" % b] + zr_all, [rg], T.DD[:, o:e],
+                   T.X[:, 0:W].indirect(T.CU[:, 128 * b + lo:128 * b + hi]), T.ZR[:, 16 * lo:16 * hi], A.subtract)
+                op("S", [rg], [rg], lambda: S.activation(T.DD[:, o:e], T.DD[:, o:e], AF.Abs))
+                return rg
+
+            lists(0)
+            rg = [gather(0, 0, 32)]
+            lists(1)
+            places(0)
+            places(1)
+            for c in range(1, 4):
+                rg.append(gather(0, 32 * c, 32 * c + 32))
+            op("T", rg + ["GM8"], ["pK0"],
+               *[mm(T.pK0[:, m:128:16], T.DD[:, m:2048:16], T.GM8[:], False, False) for m in range(15)],
+               mm(T.pK0[:, 0:128], T.DD[:, 15:2048:16], T.GMX[:], False, True))
+            for c in range(4):
+                if c < 3:
+                    rg = [gather(1, 32 * c, 32 * c + 32)]
+                else:
+                    rg = [gather(1, 96, 112), gather(1, 112, 128)]
+                op("T", rg + ["GM8"], ["pK1"],
+                   *[mm(T.pK1[32 * c:32 * c + 32, m:128:16], T.DD[:, 2048 + 512 * c + m:2560 + 512 * c:16], T.GM8[:],
+                        False, False) for m in range(15)])
+                if c == 3:
+                    op("T", rg + ["GMX"], ["pK1"], mm(T.pK1[:, 0:128], T.DD[:, 2063:W:16], T.GMX[:], False, True))
+                if c == 1:
+                    scan(["pK0", "RS"], ["R0"], T.R0[:], T.RS[:], T.pK0[:, 0:128], 0.0, A.max, A.min)
+            if d == 0:
+                lv = LL[:, 0:128]
+                ts([ll], ["RT"], T.RT[:], lv, -1.0, A.add)
+                scan([ll, "ZD0"], ["RSC"], T.RSC[:], T.ZD0[:], lv, 0.0, A.mult, A.add)
+                tt(["RSC", "PWS"], ["RW"], T.RW[:], T.RSC[:, 15:128:16], T.PWS[:, 15:128:16], A.mult)
+                if t == 1:
+                    op("T", [ll, "BOF"], ["pM"], mm(T.pM[:, 0:128], T.BOF[:], LL[:, 128:256]))
+                    tt(["FA", "pM"], ["FA"], T.FA[:, 0:W:32], T.FA[:, 0:W:32], T.pM[:, 0:128], A.add)
+            scan(["pK1", "RS"], ["R1"], T.R1[:], T.RS[:], T.pK1[:, 0:128], 0.0, A.max, A.min)
+            tt(["R0", "R1"], ["MK"], T.MK[:], T.R0[:, 15:128:16], T.R1[:, 15:128:16], A.min)
+            cp(["MK"], ["MI"], T.MI[:], T.MK[:])
+            ts(["MI", "ZSc"], ["ZS"], T.ZS[:, 0:128:16], T.MI[:], W - 1, A.bitwise_and)
+            scan(["ZS", "ZSc", "ZD0"], ["YE"], T.YE[:], T.ZD0[:], T.ZS[:], 0.0, A.mult, A.add)
+            tt(["YE", "pC"], ["YM"], T.YM[:], T.YE[:], M16P, A.mult)
+            op("T", ["YM", "SEL8"], ["pYW"], mm(T.pYW[:, 0:8], T.YM[:], T.SEL8[:]))
+            op("T", ["YE", "IDF"], ["pYR"], mm(T.pYR[:, 0:128], T.YE[:], T.IDF[:]))
+            cp(["pYW"], ["YU"], T.YU[:], T.pYW[:, 0:8])
+            tt([far, "YU", "RT"], ["EL"], T.EL[:], F[:, 0:W].indirect(T.YU[:]), T.RT[:], A.is_lt)
+            for h in (0, 7, 6, 5, 4, 3, 2, 1):
+                lo = 16 * h if h > 1 else 0
+                a, e = 128 * h + lo, 128 * h + 128
+                ts(["pYR", "pYW", "RW"], ["EQ%d" % h], T.EQ[:, a:e], T.pYR[:, lo:128], T.pYW[:, h:h + 1],
+                   A.is_equal, T.RW[:, h:h + 1], A.mult)
+                op("T", ["EQ%d" % h, "BOB"], ["pWS"], mm(T.pWS[:, lo:128], T.BOB[:], T.EQ[:, a:e], h == 0, h == 1))
+            tt(["EL", "pC"], ["TH"], T.TH[:], T.EL[:], THRP, A.mult)
+            tt(["pYW", "DW"], ["YD"], T.YD[:], T.pYW[:, 0:8], T.DW[:], A.subtract)
+            tt(["pWS", "TH"], ["WM"], T.WM[:], T.pWS[:, 0:128], T.TH[:], A.is_lt)
+            tt(["X", "YU", ss], ["XG"], T.XG[:], T.X[:, 0:W].indirect(T.YU[:]), SS[:], A.add)
+            scan(["WM", "ZD0"], ["WS"], T.WS[:], T.ZD0[:], T.WM[:], 0.0, A.mult, A.add)
+            ts(["XG"], ["NR"], T.NR[:], T.XG[:], 0.5, A.mult, -0.25, A.add)
+            won = T.WS[:, 15:128:16]
+            tt(["WS", "YD"], ["SF0"], T.SF0[:], won, T.YD[:], A.mult)
+            mu = "MU%d%d" % (t, d)
+            MU = T[mu]
+            if d < D - 1:
+                cp(["NR"], [mu + "r"], MU[:, 0:128], T.NR[:])
+            tt(["SF0", "DW"], ["SF"], T.SF[:], T.SF0[:], T.DW[:], A.add)
+            cp(["SF"], [mu], MU[:, 128:136], T.SF[:])
+            sl = MU[:, 128:136]
+
+            def far_write():
+                cp([mu, "ST%d" % t, far + "spare"], [far], F[:, 0:WX].indirect(sl), ST[:])
+
+            def rec_write():
+                cp([mu, "NR", "Xspare"], ["X"], T.X[:, 0:WX].indirect(sl), T.NR[:])
+
+            def pairs():
+                ts(["pYR"], ["Y1"], T.Y1[:], T.pYR[:, 0:128], 1.0, A.add)
+                if d == 0:
+                    tt(["WM", "Y1"], ["YN"], T.YN[:], T.WM[:], T.Y1[:], A.mult)
+                    return
+                tt(["WM", "Y1"], ["YA"], T.YA[:], T.WM[:], T.Y1[:], A.mult)
+                if d < D - 1:
+                    tt(["YN", "YA"], ["YN"], T.YN[:], T.YN[:], T.YA[:], A.add)
+                elif t == 0:
+                    tt(["YN", "YA"], ["LS1n"], T.LS1[:, 128:256], T.YN[:], T.YA[:], A.add)
+                else:
+                    tt(["YN", "YA"], ["LSF"], T.LSF[:], T.YN[:], T.YA[:], A.add)
+
+            def kappa():
+                op("V", ["WS"], ["CT"], lambda: V.tensor_reduce(T.CT[:], won, AxisListType.X, A.add))
+                op("T", ["CT", "ONF"], ["pM"], mm(T.pM[:, 0:1], T.ONF[:], T.CT[:]))
+
+            def kappa2():
+                cp(["pM"], ["KI"], T.KI[:], T.pM[:, 0:1])
+                ts(["KI"], ["KJ"], T.KJ[:], T.KI[:], 31, A.bitwise_and)
+                cp(["KJ"], ["KF"], T.KF[:], T.KJ[:])
+                ts(["KB", "KF"], ["KC"], T.KC[:], T.KB[:], T.KF[:], A.add, 97.0 * ((d + 1) % D), A.add)
+
+            if d < D - 1:
+                un = "U%d%d" % (t, d)
+                ul = "UL%d%d" % (t, d)
+                send(un, to, T[ul][:], MU[:], [mu, mu + "r"], ul)
+                far_write()
+                kappa()
+                tt([far, "YU", "M16"], ["PG"], T.PG[:], F[:, 0:W].indirect(T.YU[:]), T.M16[:], A.mult)
+                scan(["PG", "ZD0"], ["PS"], T.PS[:], T.ZD0[:], T.PG[:], 0.0, A.mult, A.add)
+                kappa2()
+                cp(["PS"], ["PU"], T.PU[:], T.PS[:, 15:128:16])
+                rec_write()
+                tt(["RT", "WM"], ["RT"], T.RT[:], T.RT[:], T.WM[:], A.subtract)
+                tt(["RW", "WS"], ["RWT"], T.RWT[:], T.RW[:], won, A.mult)
+                tt(["RW", "RWT"], ["RW"], T.RW[:], T.RW[:], T.RWT[:], A.subtract)
+                pairs()
+                cp([ul, xr + "spare"], [xr], XR[:, 0:WX].indirect(T[ul][:, 128:136]), T[ul][:, 0:128])
+                cp([xr, "PU"], ["Z"], T.Z[:], XR[:, 0:W].indirect(T.PU[:]))
+            elif t == 0:
+                rec_write()
+                cp(["X"], ["SN1"], T.SN1[:], T.X[:, 1:W:32])
+                send("S1", prv, T.SS1[:], T.SN1[:], ["SN1"], "SS1")
+                kappa()
+                far_write()
+                tt(["FB", "M16M"], ["LS1l"], T.LS1[:, 0:128], T.FB[:, 1:W:32], T.M16M[:], A.is_lt)
+                kappa2()
+                pairs()
+                send("X1", prv, T.XR1[:, 0:W], T.X[:, 0:W], ["X"], "XR1")
+                send("L1", prv, T.LL1[:], T.LS1[:], ["LS1l", "LS1n"], "LL1")
+            else:
+                pairs()
+                send("LF", home, T.LLF[:], T.LSF[:], ["LSF"], "LLF")
+                rec_write()
+                dma("Y", "oX", [(T.yx[:], T.X[:, 0:W])], ["X"], ["yx"])
+                far_write()
+                dma("Y", "oA", [(T.ya[:], T.FA[0:128:16, 0:W])], ["FA"], ["ya"])
+
+    op("T", ["LLF", "BOF"], ["pM"], mm(T.pM[:, 0:128], T.BOF[:], T.LLF[:]))
+    tt(["FB", "pM"], ["FB"], T.FB[:, 1:W:32], T.FB[:, 1:W:32], T.pM[:, 0:128], A.add)
+    dma("Y", "oB", [(T.yb[:], T.FB[0:128:16, 0:W])], ["FB"], ["yb"])
+    finish()

@@ -89,7 +89,9 @@ SCRATCH = {
     "DD": ("sbuf", [128, W], "bfloat16"),
     "R0": ("sbuf", [128, 128], "float32"),
     "R1": ("sbuf", [128, 128], "float32"),
-    "MK": ("sbuf", [128, 8], "float32"),
+    "IDB": ("sbuf", [128, 128], "bfloat16"),
+    "NIB": ("sbuf", [128, 128], "bfloat16"),
+    "GS": ("sbuf", [128, 1024], "bfloat16"),
     "MI": ("sbuf", [128, 8], "int32"),
     "ZS": ("sbuf", [128, 128], "int32"),
     "YE": ("sbuf", [128, 128], "float32"),
@@ -248,6 +250,9 @@ def rank_program(g, core, T, topo):
     def scan(reads, writes, out, d0, d1, init, o0, o1):
         op("V", reads, writes, lambda: V.tensor_tensor_scan(out, d0, d1, init, o0, o1))
 
+    def act(reads, writes, out, in_, **kw):
+        op("S", reads, writes, lambda: S.activation(out, in_, AF.Copy, **kw))
+
     def fill(writes, ap, c):
         op("V", [], writes, lambda: V.memset(ap, c))
 
@@ -262,6 +267,9 @@ def rank_program(g, core, T, topo):
 
     op("G", [], ["PI"], lambda: g.iota(T.PI[:], [[0, 1]], 0, 1))
     op("G", [], ["CI"], lambda: g.iota(T.CI[:], [[1, 128]], 0, 0))
+    for b in range(TB):
+        op("G", [], ["ST%d" % b], lambda: g.iota(T["ST%d" % b][:], [[32, 128]], b, 0,
+                                                 allow_small_or_imprecise_dtypes=True))
     fill(["ONF"], T.ONF[:], 1.0)
     fill(["HALF"], T.HALF[:], 0.5)
     fill(["ZERO"], T.ZERO[:], 0.0)
@@ -281,15 +289,15 @@ def rank_program(g, core, T, topo):
     ts(["P8"], ["LV8"], T.LV8[:], T.P8[:, 0:W:32], 0.0, A.is_lt)
     op("T", ["E8", "LV8"], ["pM"], mm(T.pM[:, 0:128], T.E8[:], T.LV8[:]))
     ts(["CGI", "PFg"], ["BOB"], T.BOB[:], T.CGI[:], PGc, A.is_equal)
-    ts(["CGI", "PFg"], ["BOF"], T.BOF[:], T.CGI[:], PGc, A.is_equal)
+    act(["BOB"], ["BOF"], T.BOF[:], T.BOB[:])
     tt(["pM", "M16"], ["LS0"], T.LS0[:], T.pM[:, 0:128], T.M16[:], A.mult)
     send("L0", nxt, T.LL0[:], T.LS0[:], ["LS0"], "LL0")
     ts(["WTI"], ["WHI"], T.WHI[:], T.WTI[:], 4032, A.bitwise_and)
     ts(["WTI"], ["WLI"], T.WLI[:], T.WTI[:], 63, A.bitwise_and)
     cp(["WHI"], ["WFh"], T.WF[:, 0:1], T.WHI[:])
     cp(["WLI"], ["WFl"], T.WF[:, 1:2], T.WLI[:])
-    ts(["BOB", "WFh"], ["WH"], T.WH[:], T.BOB[:], T.WF[:, 0:1], A.mult)
-    ts(["BOB", "WFl"], ["WL"], T.WL[:], T.BOB[:], T.WF[:, 1:2], A.mult)
+    act(["BOB", "WFh"], ["WH"], T.WH[:], T.BOB[:], scale=T.WF[:, 0:1])
+    act(["BOB", "WFl"], ["WL"], T.WL[:], T.BOB[:], scale=T.WF[:, 1:2])
     ts(["PFm"], ["BJa"], T.BJ[:, 0:1], PM, 32.0, A.mult, 16.0, A.add)
     ts(["PFm"], ["BJb"], T.BJ[:, 1:2], PM, 32.0, A.mult, 528.0, A.add)
     tt(["BJa", "BJb"], ["BJ2"], T.BJ2[:], T.BJ[:], T.BJ[:], A.mult)
@@ -304,27 +312,28 @@ def rank_program(g, core, T, topo):
     dma("Y", "dDA", [(T.da[:], T.PA2F[:])], ["PA2F"], ["da"])
     dma("Y", "dFA", [(T.FA[f:128:16, 0:W], T.da[:]) for f in range(16)], ["da"], ["FA"])
     ts(["CI", "PFp"], ["IDF"], T.IDF[:], T.CI[:], P_, A.is_equal)
-    ts(["CI", "PFp"], ["NID"], T.NID[:], T.CI[:], P_, A.is_equal, -FULL, A.mult)
+    act(["IDF"], ["IDB"], T.IDB[:], T.IDF[:])
+    act(["IDF"], ["NIB"], T.NIB[:], T.IDF[:], scale=-1.0)
+    act(["IDF"], ["NID"], T.NID[:], T.IDF[:], scale=-FULL)
     ts(["CI", "PFg"], ["SEL8"], T.SEL8[:], T.CI[:, 0:8], PGc, A.is_equal)
     ts(["CI", "PFg"], ["GM8"], T.GM8[:], T.CI[:, 0:8], PGc, A.is_equal, 4096.0, A.mult)
     ts(["CMI"], ["GMF"], T.GMF[:], T.CMI[:], 15.0, A.is_equal, 4096.0, A.mult)
     tt(["GMF", "BOF"], ["GMX"], T.GMX[:], T.GMF[:], T.BOF[:], A.mult)
-    ts(["M16"], ["M16M"], T.M16M[:], T.M16[:], -1.0, A.add)
+    act(["M16"], ["M16M"], T.M16M[:], T.M16[:], bias=-1.0)
     ts(["CMI"], ["ZD0"], T.ZD0[:], T.CMI[:], 0.0, A.is_gt)
     ts(["CMI"], ["RS0"], T.RS0[:], T.CMI[:], 0.0, A.is_equal, 1.0e8, A.mult)
-    ts(["RS0"], ["RS"], T.RS[:], T.RS0[:], -5.0e7, A.add)
+    act(["RS0"], ["RS"], T.RS[:], T.RS0[:], bias=-5.0e7)
     scan(["HALF", "ZERO"], ["PW"], T.PW[:], T.HALF[:], T.ZERO[:], 2.0 ** 64, A.mult, A.add)
-    cp(["M16"], ["pC"], T.pC[:, 0:128], T.M16[:])
-    ts(["PW"], ["pC"], T.pC[:, 128:256], T.PW[:], 2.5, A.mult)
+    act(["M16"], ["pC"], T.pC[:, 0:128], T.M16[:])
+    act(["PW"], ["pC"], T.pC[:, 128:256], T.PW[:], scale=2.5)
     tt(["PW", "M16"], ["PWM"], T.PWM[:], T.PW[:], T.M16[:], A.mult)
     scan(["PWM", "ZD0"], ["PWS"], T.PWS[:], T.ZD0[:], T.PWM[:], 0.0, A.mult, A.add)
     ts(["CI", "PFm"], ["DW0"], T.DW0[:], T.CI[:, 0:8], 16.0, A.mult, PM, A.add)
     ts(["DW0"], ["DW"], T.DW[:], T.DW0[:], float(W), A.add)
-    ts(["CI"], ["ST0"], T.ST0[:], T.CI[:], 32.0, A.mult)
-    ts(["CI"], ["ST1"], T.ST1[:], T.CI[:], 32.0, A.mult, 1.0, A.add)
 
     M16P, THRP = T.pC[:, 0:128], T.pC[:, 128:256]
 
+    later, counted, scaled = [], [], []
     for t in range(TB):
         far = "FB" if t == 0 else "FA"
         F = T[far]
@@ -351,6 +360,8 @@ def rank_program(g, core, T, topo):
                    lambda: S.activation(T.ZR[:, m:2048:16], Z[:], AF.Copy))
             for m in range(0, 4):
                 rep_v(m)
+            while counted:
+                counted.pop(0)()
             cp(["pU"], ["UI"], T.UI[:], T.pU[:, 0:128])
             ts(["UI"], ["UM"], T.UM[:], T.UI[:], W - 1, A.bitwise_and)
             cp(["UM"], ["UF"], T.UF[:], T.UM[:])
@@ -359,6 +370,8 @@ def rank_program(g, core, T, topo):
                    lambda: S.activation(T.SQ[:, 128 * b:128 * b + 128], T.UF[:], AF.Square, bias=T.BJ[:, b:b + 1]))
             for m in range(4, 8):
                 rep_v(m)
+            while scaled:
+                scaled.pop(0)()
             first = t == 0 and d == 0
             KN = "KB" if first else "KC"
 
@@ -388,39 +401,59 @@ def rank_program(g, core, T, topo):
                 op("S", [rg], [rg], lambda: S.activation(T.DD[:, o:e], T.DD[:, o:e], AF.Abs))
                 return rg
 
+            def dist(b, c, rgs, close=False):
+                pn = "pK%d" % b
+                op("T", rgs + ["GM8"], [pn], *[
+                    mm(T[pn][32 * c:32 * c + 32, m:128:16], T.DD[:, 2048 * b + 512 * c + m:2048 * b + 512 * c + 512:16],
+                       T.GM8[:], False, False) for m in range(15)])
+                if close:
+                    op("T", rgs + ["GMX"], [pn],
+                       mm(T[pn][:, 0:128], T.DD[:, 2048 * b + 15:2048 * b + 2048:16], T.GMX[:], False, True))
+
+            def gather_s(b):
+                o, e = 2048 * b + 1536, 2048 * b + 2048
+                gs = T.GS[:, 512 * b:512 * b + 512]
+                pn = "pU" if b == 0 else "pWS"
+                op("S", ["X", "CU%d" % b], ["GS%d" % b], lambda: S.activation(
+                    gs, T.X[:, 0:W].indirect(T.CU[:, 128 * b + 96:128 * b + 128]), AF.Copy))
+                rg = "DD%d_96" % b
+                return (rg, lambda: op("T", ["GS%d" % b, "IDB"], [pn], mm(T[pn][:, 0:512], T.IDB[:], gs, False, True)),
+                        lambda: op("S", [pn], [rg], lambda: S.activation(T.DD[:, o:e], T[pn][:, 0:512], AF.Abs)))
+
+            for pn in ("pU", "pWS"):
+                op("T", ["NIB"] + zr_all, [pn], mm(T[pn][:, 0:512], T.NIB[:], T.ZR[:, 1536:2048], True, False))
             lists(0)
-            rg = [gather(0, 0, 32)]
-            lists(1)
             places(0)
+            rs0, sub0, abs0 = gather_s(0)
+            sub0()
+            dist(0, 0, [gather(0, 0, 32)])
+            lists(1)
+            rs1, sub1, abs1 = gather_s(1)
             places(1)
-            for c in range(1, 4):
-                rg.append(gather(0, 32 * c, 32 * c + 32))
-            op("T", rg + ["GM8"], ["pK0"],
-               *[mm(T.pK0[:, m:128:16], T.DD[:, m:2048:16], T.GM8[:], False, False) for m in range(15)],
-               mm(T.pK0[:, 0:128], T.DD[:, 15:2048:16], T.GMX[:], False, True))
-            for c in range(4):
-                if c < 3:
-                    rg = [gather(1, 32 * c, 32 * c + 32)]
-                else:
-                    rg = [gather(1, 96, 112), gather(1, 112, 128)]
-                op("T", rg + ["GM8"], ["pK1"],
-                   *[mm(T.pK1[32 * c:32 * c + 32, m:128:16], T.DD[:, 2048 + 512 * c + m:2560 + 512 * c:16], T.GM8[:],
-                        False, False) for m in range(15)])
-                if c == 3:
-                    op("T", rg + ["GMX"], ["pK1"], mm(T.pK1[:, 0:128], T.DD[:, 2063:W:16], T.GMX[:], False, True))
-                if c == 1:
-                    scan(["pK0", "RS"], ["R0"], T.R0[:], T.RS[:], T.pK0[:, 0:128], 0.0, A.max, A.min)
+            sub1()
+            abs0()
+            dist(0, 3, [rs0])
+            if t == 1 and d == 0:
+                op("T", [ll, "BOF"], ["pM"], mm(T.pM[:, 0:128], T.BOF[:], LL[:, 128:256]))
+            dist(0, 1, [gather(0, 32, 64)])
+            dist(0, 2, [gather(0, 64, 96)], True)
+            abs1()
+            dist(1, 3, [rs1])
+            dist(1, 0, [gather(1, 0, 32)])
+            dist(1, 1, [gather(1, 32, 64)])
+            dist(1, 2, [gather(1, 64, 80), gather(1, 80, 96)], True)
             if d == 0:
                 lv = LL[:, 0:128]
                 ts([ll], ["RT"], T.RT[:], lv, -1.0, A.add)
                 scan([ll, "ZD0"], ["RSC"], T.RSC[:], T.ZD0[:], lv, 0.0, A.mult, A.add)
                 tt(["RSC", "PWS"], ["RW"], T.RW[:], T.RSC[:, 15:128:16], T.PWS[:, 15:128:16], A.mult)
                 if t == 1:
-                    op("T", [ll, "BOF"], ["pM"], mm(T.pM[:, 0:128], T.BOF[:], LL[:, 128:256]))
                     tt(["FA", "pM"], ["FA"], T.FA[:, 0:W:32], T.FA[:, 0:W:32], T.pM[:, 0:128], A.add)
+            while later:
+                later.pop()()
+            scan(["pK0", "RS"], ["R0"], T.R0[:], T.RS[:], T.pK0[:, 0:128], 0.0, A.max, A.min)
             scan(["pK1", "RS"], ["R1"], T.R1[:], T.RS[:], T.pK1[:, 0:128], 0.0, A.max, A.min)
-            tt(["R0", "R1"], ["MK"], T.MK[:], T.R0[:, 15:128:16], T.R1[:, 15:128:16], A.min)
-            cp(["MK"], ["MI"], T.MI[:], T.MK[:])
+            tt(["R0", "R1"], ["MI"], T.MI[:], T.R0[:, 15:128:16], T.R1[:, 15:128:16], A.min)
             ts(["MI", "ZSc"], ["ZS"], T.ZS[:, 0:128:16], T.MI[:], W - 1, A.bitwise_and)
             scan(["ZS", "ZSc", "ZD0"], ["YE"], T.YE[:], T.ZD0[:], T.ZS[:], 0.0, A.mult, A.add)
             tt(["YE", "pC"], ["YM"], T.YM[:], T.YE[:], M16P, A.mult)
@@ -428,24 +461,26 @@ def rank_program(g, core, T, topo):
             op("T", ["YE", "IDF"], ["pYR"], mm(T.pYR[:, 0:128], T.YE[:], T.IDF[:]))
             cp(["pYW"], ["YU"], T.YU[:], T.pYW[:, 0:8])
             tt([far, "YU", "RT"], ["EL"], T.EL[:], F[:, 0:W].indirect(T.YU[:]), T.RT[:], A.is_lt)
+            tt(["pYW", "DW"], ["YD"], T.YD[:], T.pYW[:, 0:8], T.DW[:], A.subtract)
+            tt(["EL", "pC"], ["TH"], T.TH[:], T.EL[:], THRP, A.mult)
             for h in (0, 7, 6, 5, 4, 3, 2, 1):
                 lo = 16 * h if h > 1 else 0
                 a, e = 128 * h + lo, 128 * h + 128
                 ts(["pYR", "pYW", "RW"], ["EQ%d" % h], T.EQ[:, a:e], T.pYR[:, lo:128], T.pYW[:, h:h + 1],
                    A.is_equal, T.RW[:, h:h + 1], A.mult)
                 op("T", ["EQ%d" % h, "BOB"], ["pWS"], mm(T.pWS[:, lo:128], T.BOB[:], T.EQ[:, a:e], h == 0, h == 1))
-            tt(["EL", "pC"], ["TH"], T.TH[:], T.EL[:], THRP, A.mult)
-            tt(["pYW", "DW"], ["YD"], T.YD[:], T.pYW[:, 0:8], T.DW[:], A.subtract)
-            tt(["pWS", "TH"], ["WM"], T.WM[:], T.pWS[:, 0:128], T.TH[:], A.is_lt)
             tt(["X", "YU", ss], ["XG"], T.XG[:], T.X[:, 0:W].indirect(T.YU[:]), SS[:], A.add)
-            scan(["WM", "ZD0"], ["WS"], T.WS[:], T.ZD0[:], T.WM[:], 0.0, A.mult, A.add)
             ts(["XG"], ["NR"], T.NR[:], T.XG[:], 0.5, A.mult, -0.25, A.add)
-            won = T.WS[:, 15:128:16]
-            tt(["WS", "YD"], ["SF0"], T.SF0[:], won, T.YD[:], A.mult)
             mu = "MU%d%d" % (t, d)
             MU = T[mu]
             if d < D - 1:
                 cp(["NR"], [mu + "r"], MU[:, 0:128], T.NR[:])
+            else:
+                ts(["pYR"], ["Y1"], T.Y1[:], T.pYR[:, 0:128], 1.0, A.add)
+            tt(["pWS", "TH"], ["WM"], T.WM[:], T.pWS[:, 0:128], T.TH[:], A.is_lt)
+            scan(["WM", "ZD0"], ["WS"], T.WS[:], T.ZD0[:], T.WM[:], 0.0, A.mult, A.add)
+            won = T.WS[:, 15:128:16]
+            tt(["WS", "YD"], ["SF0"], T.SF0[:], won, T.YD[:], A.mult)
             tt(["SF0", "DW"], ["SF"], T.SF[:], T.SF0[:], T.DW[:], A.add)
             cp(["SF"], [mu], MU[:, 128:136], T.SF[:])
             sl = MU[:, 128:136]
@@ -456,8 +491,9 @@ def rank_program(g, core, T, topo):
             def rec_write():
                 cp([mu, "NR", "Xspare"], ["X"], T.X[:, 0:WX].indirect(sl), T.NR[:])
 
-            def pairs():
-                ts(["pYR"], ["Y1"], T.Y1[:], T.pYR[:, 0:128], 1.0, A.add)
+            def pairs(d=d, t=t):
+                if d < D - 1:
+                    ts(["pYR"], ["Y1"], T.Y1[:], T.pYR[:, 0:128], 1.0, A.add)
                 if d == 0:
                     tt(["WM", "Y1"], ["YN"], T.YN[:], T.WM[:], T.Y1[:], A.mult)
                     return
@@ -469,15 +505,22 @@ def rank_program(g, core, T, topo):
                 else:
                     tt(["YN", "YA"], ["LSF"], T.LSF[:], T.YN[:], T.YA[:], A.add)
 
+            def after(d=d, won=won, pairs=pairs):
+                tt(["RT", "WM"], ["RT"], T.RT[:], T.RT[:], T.WM[:], A.subtract)
+                tt(["RW", "WS"], ["RWT"], T.RWT[:], T.RW[:], won, A.mult)
+                tt(["RW", "RWT"], ["RW"], T.RW[:], T.RW[:], T.RWT[:], A.subtract)
+                pairs()
+
             def kappa():
                 op("V", ["WS"], ["CT"], lambda: V.tensor_reduce(T.CT[:], won, AxisListType.X, A.add))
                 op("T", ["CT", "ONF"], ["pM"], mm(T.pM[:, 0:1], T.ONF[:], T.CT[:]))
 
             def kappa2():
-                cp(["pM"], ["KI"], T.KI[:], T.pM[:, 0:1])
-                ts(["KI"], ["KJ"], T.KJ[:], T.KI[:], 31, A.bitwise_and)
-                cp(["KJ"], ["KF"], T.KF[:], T.KJ[:])
-                ts(["KB", "KF"], ["KC"], T.KC[:], T.KB[:], T.KF[:], A.add, 97.0 * ((d + 1) % D), A.add)
+                step = 97.0 * ((d + 1) % D)
+                counted.append(lambda: cp(["pM"], ["KI"], T.KI[:], T.pM[:, 0:1]))
+                counted.append(lambda: ts(["KI"], ["KJ"], T.KJ[:], T.KI[:], 31, A.bitwise_and))
+                scaled.append(lambda: cp(["KJ"], ["KF"], T.KF[:], T.KJ[:]))
+                scaled.append(lambda: ts(["KB", "KF"], ["KC"], T.KC[:], T.KB[:], T.KF[:], A.add, step, A.add))
 
             if d < D - 1:
                 un = "U%d%d" % (t, d)
@@ -490,10 +533,7 @@ def rank_program(g, core, T, topo):
                 kappa2()
                 cp(["PS"], ["PU"], T.PU[:], T.PS[:, 15:128:16])
                 rec_write()
-                tt(["RT", "WM"], ["RT"], T.RT[:], T.RT[:], T.WM[:], A.subtract)
-                tt(["RW", "WS"], ["RWT"], T.RWT[:], T.RW[:], won, A.mult)
-                tt(["RW", "RWT"], ["RW"], T.RW[:], T.RW[:], T.RWT[:], A.subtract)
-                pairs()
+                later.append(after)
                 cp([ul, xr + "spare"], [xr], XR[:, 0:WX].indirect(T[ul][:, 128:136]), T[ul][:, 0:128])
                 cp([xr, "PU"], ["Z"], T.Z[:], XR[:, 0:W].indirect(T.PU[:]))
             elif t == 0:

from concourse.mybir import dt, AluOpType, AxisListType, ActivationFunctionType

A = AluOpType
AF = ActivationFunctionType
W, L, TB, D = 4096, 128, 2, 3
WX = W + L
FULL = 16777216.0

SCRATCH = {
    "X": ("sbuf", [128, WX], "bfloat16"),
    "XR0": ("sbuf", [128, WX], "bfloat16"),
    "XR1": ("sbuf", [128, WX], "bfloat16"),
    "FA": ("sbuf", [128, WX], "float32"),
    "FB": ("sbuf", [128, WX], "float32"),
    "P8": ("sbuf", [8, W], "int32"),
    "PA2": ("sbuf", [128, 256], "int32"),
    "PB2": ("sbuf", [128, 256], "int32"),
    "PA2F": ("sbuf", [128, 256], "float32"),
    "PB2F": ("sbuf", [128, 256], "float32"),
    "da": ("dram", [8, W], "float32"),
    "db": ("dram", [8, W], "float32"),
    "WTI": ("sbuf", [128, 1], "int32"),
    "WHI": ("sbuf", [128, 1], "int32"),
    "WLI": ("sbuf", [128, 1], "int32"),
    "WF": ("sbuf", [128, 2], "float32"),
    "WH": ("sbuf", [128, 128], "bfloat16"),
    "WL": ("sbuf", [128, 128], "bfloat16"),
    "PI": ("sbuf", [128, 1], "int32"),
    "PMI": ("sbuf", [128, 1], "int32"),
    "PGI": ("sbuf", [128, 1], "int32"),
    "PF": ("sbuf", [128, 3], "float32"),
    "CI": ("sbuf", [128, 128], "int32"),
    "CMI": ("sbuf", [128, 128], "int32"),
    "CGI": ("sbuf", [128, 128], "int32"),
    "M16": ("sbuf", [128, 128], "float32"),
    "M16M": ("sbuf", [128, 128], "float32"),
    "BOB": ("sbuf", [128, 128], "bfloat16"),
    "BOF": ("sbuf", [128, 128], "float32"),
    "IDF": ("sbuf", [128, 128], "float32"),
    "NID": ("sbuf", [128, 128], "bfloat16"),
    "ONF": ("sbuf", [128, 128], "float32"),
    "SEL8": ("sbuf", [128, 8], "float32"),
    "GM8": ("sbuf", [128, 8], "bfloat16"),
    "GMF": ("sbuf", [128, 128], "float32"),
    "GMX": ("sbuf", [128, 128], "bfloat16"),
    "E8": ("sbuf", [8, 128], "bfloat16"),
    "BJ": ("sbuf", [128, 2], "float32"),
    "BJ2": ("sbuf", [128, 2], "float32"),
    "KB": ("sbuf", [128, 2], "float32"),
    "KC": ("sbuf", [128, 2], "float32"),
    "ZD0": ("sbuf", [128, 128], "float32"),
    "RS0": ("sbuf", [128, 128], "float32"),
    "RS": ("sbuf", [128, 128], "float32"),
    "HALF": ("sbuf", [128, 128], "float32"),
    "ZERO": ("sbuf", [128, 128], "float32"),
    "PW": ("sbuf", [128, 128], "float32"),
    "PWM": ("sbuf", [128, 128], "float32"),
    "PWS": ("sbuf", [128, 128], "float32"),
    "DW0": ("sbuf", [128, 8], "float32"),
    "DW": ("sbuf", [128, 8], "float32"),
    "ST0": ("sbuf", [128, 128], "float32"),
    "ST1": ("sbuf", [128, 128], "float32"),
    "LV8": ("sbuf", [8, 128], "bfloat16"),
    "LS0": ("sbuf", [128, 128], "float32"),
    "LS1": ("sbuf", [128, 256], "float32"),
    "LSF": ("sbuf", [128, 128], "float32"),
    "LL0": ("sbuf", [128, 128], "float32"),
    "LL1": ("sbuf", [128, 256], "float32"),
    "LLF": ("sbuf", [128, 128], "float32"),
    "SN0": ("sbuf", [128, 128], "bfloat16"),
    "SN1": ("sbuf", [128, 128], "bfloat16"),
    "SS0": ("sbuf", [128, 128], "bfloat16"),
    "SS1": ("sbuf", [128, 128], "bfloat16"),
    "RT": ("sbuf", [128, 128], "float32"),
    "RSC": ("sbuf", [128, 128], "float32"),
    "RW": ("sbuf", [128, 8], "float32"),
    "RWT": ("sbuf", [128, 8], "float32"),
    "Z": ("sbuf", [128, 128], "bfloat16"),
    "ZR": ("sbuf", [128, 2048], "bfloat16"),
    "UI": ("sbuf", [128, 128], "int32"),
    "UM": ("sbuf", [128, 128], "int32"),
    "UF": ("sbuf", [128, 128], "float32"),
    "SQ": ("sbuf", [128, 256], "float32"),
    "AI": ("sbuf", [128, 256], "int32"),
    "CC": ("sbuf", [128, 256], "int32"),
    "CU": ("sbuf", [128, 256], "uint16"),
    "CF": ("sbuf", [128, 256], "float32"),
    "NQ": ("sbuf", [128, 256], "bfloat16"),
    "DD": ("sbuf", [128, W], "bfloat16"),
    "R0": ("sbuf", [128, 128], "float32"),
    "R1": ("sbuf", [128, 128], "float32"),
    "IDB": ("sbuf", [128, 128], "bfloat16"),
    "NIB": ("sbuf", [128, 128], "bfloat16"),
    "GS": ("sbuf", [128, 1024], "bfloat16"),
    "MI": ("sbuf", [128, 8], "int32"),
    "ZS": ("sbuf", [128, 128], "int32"),
    "YE": ("sbuf", [128, 128], "float32"),
    "YM": ("sbuf", [128, 128], "float32"),
    "YU": ("sbuf", [128, 8], "uint16"),
    "YD": ("sbuf", [128, 8], "float32"),
    "EL": ("sbuf", [128, 128], "float32"),
    "TH": ("sbuf", [128, 128], "float32"),
    "EQ": ("sbuf", [128, 1024], "bfloat16"),
    "XG": ("sbuf", [128, 128], "float32"),
    "NR": ("sbuf", [128, 128], "int32"),
    "WM": ("sbuf", [128, 128], "float32"),
    "WS": ("sbuf", [128, 128], "float32"),
    "SF0": ("sbuf", [128, 8], "float32"),
    "SF": ("sbuf", [128, 8], "float32"),
    "Y1": ("sbuf", [128, 128], "float32"),
    "YA": ("sbuf", [128, 128], "float32"),
    "YN": ("sbuf", [128, 128], "float32"),
    "CT": ("sbuf", [128, 1], "float32"),
    "KI": ("sbuf", [128, 1], "int32"),
    "KJ": ("sbuf", [128, 1], "int32"),
    "KF": ("sbuf", [128, 1], "float32"),
    "PG": ("sbuf", [128, 128], "float32"),
    "PS": ("sbuf", [128, 128], "float32"),
    "PU": ("sbuf", [128, 8], "uint16"),
    "pU": ("psum", [128, 512], "float32"),
    "pK0": ("psum", [128, 512], "float32"),
    "pK1": ("psum", [128, 512], "float32"),
    "pYR": ("psum", [128, 512], "float32"),
    "pYW": ("psum", [128, 512], "float32"),
    "pWS": ("psum", [128, 512], "float32"),
    "pC": ("psum", [128, 512], "float32"),
    "pM": ("psum", [128, 512], "float32"),
}
for _t in range(TB):
    for _d in range(D):
        SCRATCH["MU%d%d" % (_t, _d)] = ("sbuf", [128, 136], "uint16")
        if _d < D - 1:
            SCRATCH["UL%d%d" % (_t, _d)] = ("sbuf", [128, 136], "uint16")

REMOTE = ["L0", "S0", "X0", "U00", "U01", "S1", "L1", "X1", "U10", "U11", "LF"]
LOCAL = ["dW", "dP8", "dX", "dPB", "dPA", "dDB", "dDA", "dFB", "dFA", "oX", "oA", "oB"]
SEMAPHORES = ["qV", "qS", "qT", "qG"] + ["a" + n for n in REMOTE] + ["l" + n for n in REMOTE] + LOCAL


def machine(g, core, T, topo):
    Q = {"V": g.vector, "S": g.scalar, "T": g.tensor, "G": g, "Y": g.sync}
    sem = {"V": "qV", "S": "qS", "T": "qT", "G": "qG"}
    cnt = {}
    know = {q: {} for q in Q}
    snap = {}
    lastw = {}
    readers = {}

    def wait(q, toks):
        todo = []
        for t in toks:
            if t not in todo and know[q].get(t[0], 0) < t[1]:
                todo.append(t)
        keep = []
        for t in todo:
            covered = False
            for o in todo:
                if o != t and snap.get(o, {}).get(t[0], 0) >= t[1]:
                    covered = True
            if not covered:
                keep.append(t)
        for s, v in keep:
            if know[q].get(s, 0) >= v:
                continue
            Q[q].wait_ge(T.sem[s], v)
            know[q][s] = max(know[q].get(s, 0), v)
            for a, b in snap.get((s, v), {}).items():
                know[q][a] = max(know[q].get(a, 0), b)

    def deps(q, reads, writes):
        toks = []
        for r in reads:
            if r in lastw:
                toks.append(lastw[r][0])
        for w in writes:
            if w in lastw and not (q == "T" and lastw[w][1] == "T"):
                toks.append(lastw[w][0])
            toks.extend(readers.get(w, []))
        wait(q, toks)

    def book(q, tok, reads, writes):
        for r in reads:
            old = [t for t in readers.get(r, []) if t[0] != tok[0]]
            readers[r] = old + [tok]
        for w in writes:
            lastw[w] = (tok, q)
            readers[w] = []

    def op(q, reads, writes, *fns):
        deps(q, reads, writes)
        ins = None
        for f in fns:
            ins = f()
        cnt[sem[q]] = cnt.get(sem[q], 0) + 1
        ins.then_inc(T.sem[sem[q]], 1)
        tok = (sem[q], cnt[sem[q]])
        know_now = dict(know[q])
        know_now[sem[q]] = tok[1]
        snap[tok] = know_now
        book(q, tok, reads, writes)

    def dma(q, name, pairs, reads, writes):
        deps(q, reads, writes)
        for o, i in pairs:
            Q[q].dma_start(o, i).then_inc(T.sem[name], 16)
        cnt[name] = 16 * len(pairs)
        tok = (name, cnt[name])
        snap[tok] = dict(know[q])
        book(q, tok, reads, writes)

    def send(name, dst, out, src, reads, lands):
        deps("G", reads, [])
        rid, pid = topo.addr(dst)[0], topo.addr(dst)[1]
        g.remote_dma(out_ap=out, in_ap=src, remote_sem=T.sem["a" + name], local_sem=T.sem["l" + name],
                     pid=pid, routing_id=rid, dma_engine_mask=topo.mask(core, dst))
        n = len(topo.engines(core, dst))
        cnt["l" + name] = n
        cnt["a" + name] = n
        book("G", ("l" + name, n), reads, [])
        lastw[lands] = (("a" + name, n), "R")
        readers[lands] = []

    def finish():
        wait("G", [(s, n) for s, n in cnt.items()])

    return op, dma, send, finish


def rank_program(g, core, T, topo):
    rank = T.rank_of(core)
    if rank is None:
        return
    N = len(T.cores)
    nxt, prv = T.cores[(rank + 1) % N], T.cores[(rank - 1) % N]
    op, dma, send, finish = machine(g, core, T, topo)
    V, S, TE = g.vector, g.scalar, g.tensor

    def ts(reads, writes, out, in0, s1, o0, s2=None, o1=None):
        if o1 is None:
            op("V", reads, writes, lambda: V.tensor_scalar(out, in0, s1, None, o0))
        else:
            op("V", reads, writes, lambda: V.tensor_scalar(out, in0, s1, s2, o0, o1))

    def tt(reads, writes, out, in0, in1, o):
        op("V", reads, writes, lambda: V.tensor_tensor(out, in0, in1, o))

    def cp(reads, writes, out, in_):
        op("V", reads, writes, lambda: V.tensor_copy(out, in_))

    def scan(reads, writes, out, d0, d1, init, o0, o1):
        op("V", reads, writes, lambda: V.tensor_tensor_scan(out, d0, d1, init, o0, o1))

    def act(reads, writes, out, in_, **kw):
        op("S", reads, writes, lambda: S.activation(out, in_, AF.Copy, **kw))

    def fill(writes, ap, c):
        op("V", [], writes, lambda: V.memset(ap, c))

    def mm(out, lhsT, rhs, start=True, stop=True):
        return lambda: TE.matmul(out, lhsT, rhs, start, stop)

    dma("Y", "dP8", [(T.P8[:], T.pa[:])], [], ["P8"])
    dma("Y", "dX", [(T.X[:, 0:W], T.x[:])], [], ["X"])
    dma("Y", "dW", [(T.WTI[:], T.wt[:])], [], ["WTI"])
    dma("Y", "dPB", [(T.PB2[:], T.pb[:])], [], ["PB2"])
    dma("Y", "dPA", [(T.PA2[:], T.pa[:])], [], ["PA2"])

    op("G", [], ["PI"], lambda: g.iota(T.PI[:], [[0, 1]], 0, 1))
    op("G", [], ["CI"], lambda: g.iota(T.CI[:], [[1, 128]], 0, 0))
    for b in range(TB):
        op("G", [], ["ST%d" % b], lambda: g.iota(T["ST%d" % b][:], [[32, 128]], b, 0,
                                                 allow_small_or_imprecise_dtypes=True))
    fill(["ONF"], T.ONF[:], 1.0)
    fill(["HALF"], T.HALF[:], 0.5)
    fill(["ZERO"], T.ZERO[:], 0.0)
    fill(["ZSc"], T.ZS[:], 0)
    for n in ("X", "XR0", "XR1", "FA", "FB"):
        fill([n + "spare"], T[n][:, W:WX], 0.0)
    ts(["PI"], ["PMI"], T.PMI[:], T.PI[:], 15, A.bitwise_and)
    ts(["PI"], ["PGI"], T.PGI[:], T.PI[:], 4, A.logical_shift_right)
    ts(["CI"], ["CMI"], T.CMI[:], T.CI[:], 15, A.bitwise_and)
    ts(["CI"], ["CGI"], T.CGI[:], T.CI[:], 4, A.logical_shift_right)
    cp(["PI"], ["PFp"], T.PF[:, 0:1], T.PI[:])
    cp(["PMI"], ["PFm"], T.PF[:, 1:2], T.PMI[:])
    cp(["PGI"], ["PFg"], T.PF[:, 2:3], T.PGI[:])
    P_, PM, PGc = T.PF[:, 0:1], T.PF[:, 1:2], T.PF[:, 2:3]
    ts(["CGI", "PFp"], ["E8"], T.E8[:], T.CGI[0:8, :], T.PF[0:8, 0:1], A.is_equal)
    ts(["CMI", "PFm"], ["M16"], T.M16[:], T.CMI[:], PM, A.is_equal)
    ts(["P8"], ["LV8"], T.LV8[:], T.P8[:, 0:W:32], 0.0, A.is_lt)
    op("T", ["E8", "LV8"], ["pM"], mm(T.pM[:, 0:128], T.E8[:], T.LV8[:]))
    ts(["CGI", "PFg"], ["BOB"], T.BOB[:], T.CGI[:], PGc, A.is_equal)
    act(["BOB"], ["BOF"], T.BOF[:], T.BOB[:])
    tt(["pM", "M16"], ["LS0"], T.LS0[:], T.pM[:, 0:128], T.M16[:], A.mult)
    send("L0", nxt, T.LL0[:], T.LS0[:], ["LS0"], "LL0")
    ts(["WTI"], ["WHI"], T.WHI[:], T.WTI[:], 4032, A.bitwise_and)
    ts(["WTI"], ["WLI"], T.WLI[:], T.WTI[:], 63, A.bitwise_and)
    cp(["WHI"], ["WFh"], T.WF[:, 0:1], T.WHI[:])
    cp(["WLI"], ["WFl"], T.WF[:, 1:2], T.WLI[:])
    act(["BOB", "WFh"], ["WH"], T.WH[:], T.BOB[:], scale=T.WF[:, 0:1])
    act(["BOB", "WFl"], ["WL"], T.WL[:], T.BOB[:], scale=T.WF[:, 1:2])
    ts(["PFm"], ["BJa"], T.BJ[:, 0:1], PM, 32.0, A.mult, 16.0, A.add)
    ts(["PFm"], ["BJb"], T.BJ[:, 1:2], PM, 32.0, A.mult, 528.0, A.add)
    tt(["BJa", "BJb"], ["BJ2"], T.BJ2[:], T.BJ[:], T.BJ[:], A.mult)
    ts(["BJ2"], ["KB"], T.KB[:], T.BJ2[:], -1.0 / 32, A.mult, -0.4375, A.add)
    cp(["X"], ["SN0"], T.SN0[:], T.X[:, 0:W:32])
    send("S0", nxt, T.SS0[:], T.SN0[:], ["SN0"], "SS0")
    send("X0", nxt, T.XR0[:, 0:W], T.X[:, 0:W], ["X"], "XR0")
    cp(["PB2"], ["PB2F"], T.PB2F[:], T.PB2[:])
    cp(["PA2"], ["PA2F"], T.PA2F[:], T.PA2[:])
    dma("Y", "dDB", [(T.db[:], T.PB2F[:])], ["PB2F"], ["db"])
    dma("Y", "dFB", [(T.FB[f:128:16, 0:W], T.db[:]) for f in range(16)], ["db"], ["FB"])
    dma("Y", "dDA", [(T.da[:], T.PA2F[:])], ["PA2F"], ["da"])
    dma("Y", "dFA", [(T.FA[f:128:16, 0:W], T.da[:]) for f in range(16)], ["da"], ["FA"])
    ts(["CI", "PFp"], ["IDF"], T.IDF[:], T.CI[:], P_, A.is_equal)
    act(["IDF"], ["IDB"], T.IDB[:], T.IDF[:])
    act(["IDF"], ["NIB"], T.NIB[:], T.IDF[:], scale=-1.0)
    act(["IDF"], ["NID"], T.NID[:], T.IDF[:], scale=-FULL)
    ts(["CI", "PFg"], ["SEL8"], T.SEL8[:], T.CI[:, 0:8], PGc, A.is_equal)
    ts(["CI", "PFg"], ["GM8"], T.GM8[:], T.CI[:, 0:8], PGc, A.is_equal, 4096.0, A.mult)
    ts(["CMI"], ["GMF"], T.GMF[:], T.CMI[:], 15.0, A.is_equal, 4096.0, A.mult)
    tt(["GMF", "BOF"], ["GMX"], T.GMX[:], T.GMF[:], T.BOF[:], A.mult)
    act(["M16"], ["M16M"], T.M16M[:], T.M16[:], bias=-1.0)
    ts(["CMI"], ["ZD0"], T.ZD0[:], T.CMI[:], 0.0, A.is_gt)
    ts(["CMI"], ["RS0"], T.RS0[:], T.CMI[:], 0.0, A.is_equal, 1.0e8, A.mult)
    act(["RS0"], ["RS"], T.RS[:], T.RS0[:], bias=-5.0e7)
    scan(["HALF", "ZERO"], ["PW"], T.PW[:], T.HALF[:], T.ZERO[:], 2.0 ** 64, A.mult, A.add)
    act(["M16"], ["pC"], T.pC[:, 0:128], T.M16[:])
    act(["PW"], ["pC"], T.pC[:, 128:256], T.PW[:], scale=2.5)
    tt(["PW", "M16"], ["PWM"], T.PWM[:], T.PW[:], T.M16[:], A.mult)
    scan(["PWM", "ZD0"], ["PWS"], T.PWS[:], T.ZD0[:], T.PWM[:], 0.0, A.mult, A.add)
    ts(["CI", "PFm"], ["DW0"], T.DW0[:], T.CI[:, 0:8], 16.0, A.mult, PM, A.add)
    ts(["DW0"], ["DW"], T.DW[:], T.DW0[:], float(W), A.add)

    M16P, THRP = T.pC[:, 0:128], T.pC[:, 128:256]

    later, counted, scaled = [], [], []
    for t in range(TB):
        far = "FB" if t == 0 else "FA"
        F = T[far]
        xr = "XR%d" % t
        XR = T[xr]
        ss = "SS%d" % t
        SS = T[ss]
        ll = "LL%d" % t
        LL = T[ll]
        ST = T["ST%d" % t]
        to = nxt if t == 0 else prv
        home = prv if t == 0 else nxt
        for d in range(D):
            zn = ss if d == 0 else "Z"
            Z = T[zn]
            op("T", ["WH", "WL", zn], ["pU"], mm(T.pU[:, 0:128], T.WH[:], Z[:], True, False),
               mm(T.pU[:, 0:128], T.WL[:], Z[:], False, True))

            def rep_v(m):
                cp([zn], ["ZR%d" % m], T.ZR[:, m:2048:16], Z[:])

            for m in range(8, 16):
                op("S", [zn], ["ZR%d" % m],
                   lambda: S.activation(T.ZR[:, m:2048:16], Z[:], AF.Copy))
            for m in range(0, 4):
                rep_v(m)
            while counted:
                counted.pop(0)()
            cp(["pU"], ["UI"], T.UI[:], T.pU[:, 0:128])
            ts(["UI"], ["UM"], T.UM[:], T.UI[:], W - 1, A.bitwise_and)
            cp(["UM"], ["UF"], T.UF[:], T.UM[:])
            for b in range(2):
                op("S", ["UF", "BJa", "BJb"], ["SQ%d" % b],
                   lambda: S.activation(T.SQ[:, 128 * b:128 * b + 128], T.UF[:], AF.Square, bias=T.BJ[:, b:b + 1]))
            for m in range(4, 8):
                rep_v(m)
            while scaled:
                scaled.pop(0)()
            first = t == 0 and d == 0
            KN = "KB" if first else "KC"

            def lists(b):
                c = slice(128 * b, 128 * b + 128)
                ts(["SQ%d" % b, KN], ["AI%d" % b], T.AI[:, c], T.SQ[:, c], 1.0 / 32, A.mult, T[KN][:, b:b + 1], A.add)
                ts(["AI%d" % b], ["CC%d" % b], T.CC[:, c], T.AI[:, c], W - 1, A.bitwise_and)
                cp(["CC%d" % b], ["CU%d" % b], T.CU[:, c], T.CC[:, c])

            def places(b):
                c = slice(128 * b, 128 * b + 128)
                cp(["CC%d" % b], ["CF%d" % b], T.CF[:, c], T.CC[:, c])
                if d > 0:
                    tt(["CC%d" % b, "pYR"], ["NQ%d" % b], T.NQ[:, c], T.CC[:, c], T.pYR[:, 0:128], A.not_equal)
                pk = T["pK%d" % b]
                op("T", ["CF%d" % b, "IDF"], ["pK%d" % b], mm(pk[:, 0:128], T.CF[:, c], T.IDF[:], True, False))
                if d > 0:
                    op("T", ["NQ%d" % b, "NID"], ["pK%d" % b], mm(pk[:, 0:128], T.NQ[:, c], T.NID[:], False, False))

            zr_all = ["ZR%d" % m for m in range(16)]

            def gather(b, lo, hi):
                o, e = 2048 * b + 16 * lo, 2048 * b + 16 * hi
                rg = "DD%d_%d" % (b, lo)
                tt(["X", "CU%d" % b] + zr_all, [rg], T.DD[:, o:e],
                   T.X[:, 0:W].indirect(T.CU[:, 128 * b + lo:128 * b + hi]), T.ZR[:, 16 * lo:16 * hi], A.subtract)
                op("S", [rg], [rg], lambda: S.activation(T.DD[:, o:e], T.DD[:, o:e], AF.Abs))
                return rg

            def dist(b, c, rgs, close=False):
                pn = "pK%d" % b
                op("T", rgs + ["GM8"], [pn], *[
                    mm(T[pn][32 * c:32 * c + 32, m:128:16], T.DD[:, 2048 * b + 512 * c + m:2048 * b + 512 * c + 512:16],
                       T.GM8[:], False, False) for m in range(15)])
                if close:
                    op("T", rgs + ["GMX"], [pn],
                       mm(T[pn][:, 0:128], T.DD[:, 2048 * b + 15:2048 * b + 2048:16], T.GMX[:], False, True))

            def gather_s(b):
                o, e = 2048 * b + 1536, 2048 * b + 2048
                gs = T.GS[:, 512 * b:512 * b + 512]
                pn = "pU" if b == 0 else "pWS"
                op("S", ["X", "CU%d" % b], ["GS%d" % b], lambda: S.activation(
                    gs, T.X[:, 0:W].indirect(T.CU[:, 128 * b + 96:128 * b + 128]), AF.Copy))
                rg = "DD%d_96" % b
                return (rg, lambda: op("T", ["GS%d" % b, "IDB"], [pn], mm(T[pn][:, 0:512], T.IDB[:], gs, False, True)),
                        lambda: op("S", [pn], [rg], lambda: S.activation(T.DD[:, o:e], T[pn][:, 0:512], AF.Abs)))

            for pn in ("pU", "pWS"):
                op("T", ["NIB"] + zr_all, [pn], mm(T[pn][:, 0:512], T.NIB[:], T.ZR[:, 1536:2048], True, False))
            lists(0)
            places(0)
            rs0, sub0, abs0 = gather_s(0)
            sub0()
            dist(0, 0, [gather(0, 0, 32)])
            lists(1)
            rs1, sub1, abs1 = gather_s(1)
            places(1)
            sub1()
            abs0()
            dist(0, 3, [rs0])
            if t == 1 and d == 0:
                op("T", [ll, "BOF"], ["pM"], mm(T.pM[:, 0:128], T.BOF[:], LL[:, 128:256]))
            dist(0, 1, [gather(0, 32, 64)])
            dist(0, 2, [gather(0, 64, 96)], True)
            abs1()
            dist(1, 3, [rs1])
            dist(1, 0, [gather(1, 0, 32)])
            dist(1, 1, [gather(1, 32, 64)])
            dist(1, 2, [gather(1, 64, 80), gather(1, 80, 96)], True)
            if d == 0:
                lv = LL[:, 0:128]
                ts([ll], ["RT"], T.RT[:], lv, -1.0, A.add)
                scan([ll, "ZD0"], ["RSC"], T.RSC[:], T.ZD0[:], lv, 0.0, A.mult, A.add)
                tt(["RSC", "PWS"], ["RW"], T.RW[:], T.RSC[:, 15:128:16], T.PWS[:, 15:128:16], A.mult)
                if t == 1:
                    tt(["FA", "pM"], ["FA"], T.FA[:, 0:W:32], T.FA[:, 0:W:32], T.pM[:, 0:128], A.add)
            while later:
                later.pop()()
            scan(["pK0", "RS"], ["R0"], T.R0[:], T.RS[:], T.pK0[:, 0:128], 0.0, A.max, A.min)
            scan(["pK1", "RS"], ["R1"], T.R1[:], T.RS[:], T.pK1[:, 0:128], 0.0, A.max, A.min)
            tt(["R0", "R1"], ["MI"], T.MI[:], T.R0[:, 15:128:16], T.R1[:, 15:128:16], A.min)
            ts(["MI", "ZSc"], ["ZS"], T.ZS[:, 0:128:16], T.MI[:], W - 1, A.bitwise_and)
            scan(["ZS", "ZSc", "ZD0"], ["YE"], T.YE[:], T.ZD0[:], T.ZS[:], 0.0, A.mult, A.add)
            tt(["YE", "pC"], ["YM"], T.YM[:], T.YE[:], M16P, A.mult)
            op("T", ["YM", "SEL8"], ["pYW"], mm(T.pYW[:, 0:8], T.YM[:], T.SEL8[:]))
            op("T", ["YE", "IDF"], ["pYR"], mm(T.pYR[:, 0:128], T.YE[:], T.IDF[:]))
            cp(["pYW"], ["YU"], T.YU[:], T.pYW[:, 0:8])
            tt([far, "YU", "RT"], ["EL"], T.EL[:], F[:, 0:W].indirect(T.YU[:]), T.RT[:], A.is_lt)
            tt(["pYW", "DW"], ["YD"], T.YD[:], T.pYW[:, 0:8], T.DW[:], A.subtract)
            tt(["EL", "pC"], ["TH"], T.TH[:], T.EL[:], THRP, A.mult)
            for h in (0, 7, 6, 5, 4, 3, 2, 1):
                lo = 16 * h if h > 1 else 0
                a, e = 128 * h + lo, 128 * h + 128
                ts(["pYR", "pYW", "RW"], ["EQ%d" % h], T.EQ[:, a:e], T.pYR[:, lo:128], T.pYW[:, h:h + 1],
                   A.is_equal, T.RW[:, h:h + 1], A.mult)
                op("T", ["EQ%d" % h, "BOB"], ["pWS"], mm(T.pWS[:, lo:128], T.BOB[:], T.EQ[:, a:e], h == 0, h == 1))
            tt(["X", "YU", ss], ["XG"], T.XG[:], T.X[:, 0:W].indirect(T.YU[:]), SS[:], A.add)
            ts(["XG"], ["NR"], T.NR[:], T.XG[:], 0.5, A.mult, -0.25, A.add)
            mu = "MU%d%d" % (t, d)
            MU = T[mu]
            if d < D - 1:
                cp(["NR"], [mu + "r"], MU[:, 0:128], T.NR[:])
            else:
                ts(["pYR"], ["Y1"], T.Y1[:], T.pYR[:, 0:128], 1.0, A.add)
            tt(["pWS", "TH"], ["WM"], T.WM[:], T.pWS[:, 0:128], T.TH[:], A.is_lt)
            scan(["WM", "ZD0"], ["WS"], T.WS[:], T.ZD0[:], T.WM[:], 0.0, A.mult, A.add)
            won = T.WS[:, 15:128:16]
            tt(["WS", "YD"], ["SF0"], T.SF0[:], won, T.YD[:], A.mult)
            tt(["SF0", "DW"], ["SF"], T.SF[:], T.SF0[:], T.DW[:], A.add)
            cp(["SF"], [mu], MU[:, 128:136], T.SF[:])
            sl = MU[:, 128:136]

            def far_write():
                cp([mu, "ST%d" % t, far + "spare"], [far], F[:, 0:WX].indirect(sl), ST[:])

            def rec_write():
                cp([mu, "NR", "Xspare"], ["X"], T.X[:, 0:WX].indirect(sl), T.NR[:])

            def pairs(d=d, t=t):
                if d < D - 1:
                    ts(["pYR"], ["Y1"], T.Y1[:], T.pYR[:, 0:128], 1.0, A.add)
                if d == 0:
                    tt(["WM", "Y1"], ["YN"], T.YN[:], T.WM[:], T.Y1[:], A.mult)
                    return
                tt(["WM", "Y1"], ["YA"], T.YA[:], T.WM[:], T.Y1[:], A.mult)
                if d < D - 1:
                    tt(["YN", "YA"], ["YN"], T.YN[:], T.YN[:], T.YA[:], A.add)
                elif t == 0:
                    tt(["YN", "YA"], ["LS1n"], T.LS1[:, 128:256], T.YN[:], T.YA[:], A.add)
                else:
                    tt(["YN", "YA"], ["LSF"], T.LSF[:], T.YN[:], T.YA[:], A.add)

            def after(d=d, won=won, pairs=pairs):
                tt(["RT", "WM"], ["RT"], T.RT[:], T.RT[:], T.WM[:], A.subtract)
                tt(["RW", "WS"], ["RWT"], T.RWT[:], T.RW[:], won, A.mult)
                tt(["RW", "RWT"], ["RW"], T.RW[:], T.RW[:], T.RWT[:], A.subtract)
                pairs()

            def kappa():
                op("V", ["WS"], ["CT"], lambda: V.tensor_reduce(T.CT[:], won, AxisListType.X, A.add))
                op("T", ["CT", "ONF"], ["pM"], mm(T.pM[:, 0:1], T.ONF[:], T.CT[:]))

            def kappa2():
                step = 97.0 * ((d + 1) % D)
                counted.append(lambda: cp(["pM"], ["KI"], T.KI[:], T.pM[:, 0:1]))
                counted.append(lambda: ts(["KI"], ["KJ"], T.KJ[:], T.KI[:], 31, A.bitwise_and))
                scaled.append(lambda: cp(["KJ"], ["KF"], T.KF[:], T.KJ[:]))
                scaled.append(lambda: ts(["KB", "KF"], ["KC"], T.KC[:], T.KB[:], T.KF[:], A.add, step, A.add))

            if d < D - 1:
                un = "U%d%d" % (t, d)
                ul = "UL%d%d" % (t, d)
                send(un, to, T[ul][:], MU[:], [mu, mu + "r"], ul)
                far_write()
                kappa()
                tt([far, "YU", "M16"], ["PG"], T.PG[:], F[:, 0:W].indirect(T.YU[:]), T.M16[:], A.mult)
                scan(["PG", "ZD0"], ["PS"], T.PS[:], T.ZD0[:], T.PG[:], 0.0, A.mult, A.add)
                kappa2()
                cp(["PS"], ["PU"], T.PU[:], T.PS[:, 15:128:16])
                rec_write()
                later.append(after)
                cp([ul, xr + "spare"], [xr], XR[:, 0:WX].indirect(T[ul][:, 128:136]), T[ul][:, 0:128])
                cp([xr, "PU"], ["Z"], T.Z[:], XR[:, 0:W].indirect(T.PU[:]))
            elif t == 0:
                rec_write()
                cp(["X"], ["SN1"], T.SN1[:], T.X[:, 1:W:32])
                send("S1", prv, T.SS1[:], T.SN1[:], ["SN1"], "SS1")
                kappa()
                far_write()
                tt(["FB", "M16M"], ["LS1l"], T.LS1[:, 0:128], T.FB[:, 1:W:32], T.M16M[:], A.is_lt)
                kappa2()
                pairs()
                send("X1", prv, T.XR1[:, 0:W], T.X[:, 0:W], ["X"], "XR1")
                send("L1", prv, T.LL1[:], T.LS1[:], ["LS1l", "LS1n"], "LL1")
            else:
                pairs()
                send("LF", home, T.LLF[:], T.LSF[:], ["LSF"], "LLF")
                rec_write()
                dma("Y", "oX", [(T.yx[:], T.X[:, 0:W])], ["X"], ["yx"])
                far_write()
                dma("Y", "oA", [(T.ya[:], T.FA[0:128:16, 0:W])], ["FA"], ["ya"])

    op("T", ["LLF", "BOF"], ["pM"], mm(T.pM[:, 0:128], T.BOF[:], T.LLF[:]))
    tt(["FB", "pM"], ["FB"], T.FB[:, 1:W:32], T.FB[:, 1:W:32], T.pM[:, 0:128], A.add)
    dma("Y", "oB", [(T.yb[:], T.FB[0:128:16, 0:W])], ["FB"], ["yb"])
    finish()
